import numpy as np
import ml_dtypes


def mxq(x, axis, fmt="e4m3"):
    dtype, down = {"e4m3": (ml_dtypes.float8_e4m3fn, 7), "e5m2": (ml_dtypes.float8_e5m2, 14)}[fmt]
    v = np.moveaxis(np.asarray(x, np.float32).astype(ml_dtypes.bfloat16).astype(np.float64), axis, -1)
    blocks = v.reshape(v.shape[:-1] + (-1, 32))
    amax = np.abs(blocks).max(-1, keepdims=True)
    byte = np.maximum(np.where(amax > 0, np.frexp(amax)[1] - 1 + 127, 0) - down, 1)
    scale = np.exp2(byte - 127.0)
    codes = (blocks / scale).astype(np.float32).astype(dtype).astype(np.float64)
    return np.moveaxis((codes * scale).reshape(v.shape), -1, axis)


WIDE = False


def mx_kscale(k):
    if not WIDE:
        return np.ones(k)
    levels = np.array([10, -10, 5, -5, 0])
    if k % 512:
        return np.exp2(np.random.permutation(np.resize(levels, k // 32))).repeat(32)
    a = np.empty((k // 512, 16))
    for p in range(k // 512):
        a[p, :8] = np.random.permutation(np.resize(levels, 8))
        for g in range(8):
            far = levels[np.abs(levels - a[p, g]) >= 10]
            a[p, g + 8] = far[np.random.randint(len(far))]
    return np.exp2(a.ravel()).repeat(32)


def f64(x):
    return np.asarray(x).astype(np.float64)


def striped(idx):
    return np.tile(idx.reshape(-1, 16).T, (8, 1)).astype(np.uint16)


def unstriped(offs):
    return offs[:16].T.reshape(-1).astype(np.int64)


E2M1 = np.array([0.0, 0.5, 1.0, 1.5, 2.0, 3.0, 4.0, 6.0, -0.0, -0.5, -1.0, -1.5, -2.0, -3.0, -4.0, -6.0])


def pack_weight(w, fmt):
    k, n = w.shape
    w = f64(np.asarray(w, np.float32).astype(ml_dtypes.bfloat16)).reshape(k // 32, 32, n)
    amax = np.abs(w).max(1)
    if fmt == "e4m3":
        byte = np.frexp(amax)[1] - 1 + 127 - 7
    else:
        mant, ex = np.frexp(amax / 6.0)
        byte = np.where(mant > 0.5, ex, ex - 1) + 127
    byte = np.clip(np.where(amax > 0, byte, 1), 1, 254)
    scaled = (w * np.exp2(127.0 - byte)[:, None, :]).reshape(k, n).astype(np.float32)
    by_word = np.ascontiguousarray(scaled.reshape(k // 512, 128, 4, n).transpose(0, 1, 3, 2))
    if fmt == "e4m3":
        words = by_word.astype(ml_dtypes.float8_e4m3fn).view(np.uint8)
    else:
        c = by_word.astype(ml_dtypes.float4_e2m1fn).view(np.uint8) & 0xF
        words = (c[..., 0::2] | (c[..., 1::2] << 4)).reshape(k // 512, 128, 2 * n)
    return np.ascontiguousarray(words), np.ascontiguousarray(byte.astype(np.uint8).reshape(k // 512, 16, n))


def unpack_weight(words, scales, fmt):
    g, _, n = scales.shape
    words = np.ascontiguousarray(words).reshape(g, 128, n, -1)
    if fmt == "e4m3":
        vals = words.view(ml_dtypes.float8_e4m3fn).astype(np.float64)
    else:
        nib = np.empty((g, 128, n, 4), np.uint8)
        nib[..., 0::2] = words & 0xF
        nib[..., 1::2] = words >> 4
        vals = E2M1[nib]
    vals = vals * np.repeat(np.exp2(scales.astype(np.float64) - 127.0), 8, axis=1)[..., None]
    return vals.transpose(0, 1, 3, 2).reshape(g * 512, n)


def gelu(v):
    return 0.5 * v * (1.0 + np.tanh(np.sqrt(2.0 / np.pi) * (v + 0.044715 * v**3)))


K, T, E, C, N = 2560, 768, 6, 128, 128
TOP = 3
PAD = 64
K8 = 1024


def by_expert(wq, xq):
    return np.concatenate([wq[e].T @ xq[:, e * C:(e + 1) * C] for e in range(E)], axis=1)


def setup_inputs():
    n = np.random.standard_normal
    s = mx_kscale(K)[:, None]
    slot_token = np.empty(E * C, np.int64); pos = np.tile(E * C + np.arange(T) % PAD, (TOP, 1)); taken = np.zeros(T, np.int64)
    liked = np.random.randn(T)
    for e in np.random.permutation(E):
        free = np.flatnonzero(taken < TOP); pick = np.random.permutation(free[np.argsort(-(liked[free] + np.random.gumbel(size=free.size)))[:C]]); slot_token[e * C:(e + 1) * C] = pick
        pos[taken[pick], pick] = e * C + np.arange(C); taken[pick] += 1
    g = np.random.uniform(0.2, 0.8, (TOP, T))
    w = n((E, K, N)) / np.sqrt(K) / s[None]
    w8 = [pack_weight(m[:K8], "e4m3") for m in w]
    w4 = [pack_weight(m[K8:], "e2m1") for m in w]
    return {
        "xT": (n((K, T)) * s).astype(np.float32),
        "w8_words": np.stack([m[0] for m in w8]),
        "w8_scales": np.stack([m[1] for m in w8]),
        "w4_words": np.stack([m[0] for m in w4]),
        "w4_scales": np.stack([m[1] for m in w4]),
        "b": (0.3 * n((N, E))).astype(np.float32),
        "gate": np.stack([np.tile(r, (N, 1)) for r in g]).astype(np.float32),
        "offs": striped(slot_token),
        "pos1": striped(pos[0]),
        "pos2": striped(pos[1]),
        "pos3": striped(pos[2]),
    }


def reference(xT, w8_words, w8_scales, w4_words, w4_scales, b, gate, offs, pos1, pos2, pos3):
    idx = unstriped(offs)
    w = np.stack([np.concatenate([unpack_weight(w8_words[e], w8_scales[e], "e4m3"), unpack_weight(w4_words[e], w4_scales[e], "e2m1")]) for e in range(E)])
    xq = mxq(f64(xT)[:, idx], 0, "e4m3")
    y = by_expert(w, xq)
    y = gelu(y + np.repeat(f64(b), C, axis=1))
    y = np.concatenate([y, np.zeros((N, PAD))], axis=1)
    return sum(f64(gate[r]) * y[:, unstriped(p)] for r, p in enumerate((pos1, pos2, pos3)))

@@ -1,0 +1,181 @@
+from contextlib import ExitStack
+
+import concourse.mybir as mybir
+
+K, T, E, C, N = 2560, 768, 6, 128, 128
+TOP, PAD, K8 = 3, 64, 1024
+S = E * C
+FLOPS = 2 * K * S * N
+
+F32 = mybir.dt.float32
+BF16 = mybir.dt.bfloat16
+I32 = mybir.dt.int32
+U32 = mybir.dt.uint32
+U16 = mybir.dt.uint16
+U8 = mybir.dt.uint8
+FP8X4 = mybir.dt.float8_e4m3fn_x4
+FP4X4 = mybir.dt.float4_e2m1fn_x4
+GELU = mybir.ActivationFunctionType.Gelu_apprx_tanh
+MULT = mybir.AluOpType.mult
+ADD = mybir.AluOpType.add
+
+P = 128
+PASSES8, PASSES4 = 2, 3
+PASSES = 5
+CHUNK = 256
+CHUNKS = T // CHUNK
+WINDOW = 1024
+ORDER = [("e2m1", 0, 0, 0), ("e2m1", 1, 1, 0), ("e2m1", 2, 2, 0), ("e4m3", 0, 2, 4), ("e4m3", 1, 2, 8)]
+LAST_GROUPS = [(0, 3), (3, 5), (5, 6)]
+OUT_PARTS = [(0, 512), (512, 768)]
+
+
+def tile_moe_ecr_lin_gelu_kernel(
+    tc, xT, w8_words, w8_scales, w4_words, w4_scales, b, gate, offs, pos1, pos2, pos3, out
+):
+    nc = tc.nc
+    with ExitStack() as ctx:
+        keep = ctx.enter_context(tc.tile_pool(name="keep", bufs=1))
+        psum = ctx.enter_context(tc.psum_pool(name="psum", bufs=1))
+
+        offs_sb = keep.tile([P, S // 16], U16, name="offs_sb")
+        pos_sb = [keep.tile([P, T // 16], U16, name="pos_sb%d" % r) for r in range(TOP)]
+        bias = keep.tile([P, E], F32, name="bias")
+        gate_sb = [keep.tile([P, T], F32, name="gate_sb%d" % r) for r in range(TOP)]
+        w8_sb = [keep.tile([P, E, 4 * N], U8, name="w8_sb%d" % a, align_bytes=64) for a in range(PASSES8)]
+        w4_sb = [keep.tile([P, E, 2 * N], U8, name="w4_sb%d" % a, align_bytes=64) for a in range(PASSES4)]
+        w8_sc = keep.tile([P, E * PASSES8, N], U8, name="w8_sc", align_bytes=64)
+        w4_sc = keep.tile([P, E * PASSES4, N], U8, name="w4_sc", align_bytes=64)
+        raw = [[keep.tile([P, 4, CHUNK], F32, name="raw%d_%d" % (s, c)) for c in range(CHUNKS)] for s in range(PASSES)]
+        grouped = [[keep.tile([P, CHUNK, 4], BF16, name="grouped%d_%d" % (s, c), align_bytes=64) for c in range(CHUNKS)] for s in range(PASSES)]
+        tok_words = keep.tile([P, PASSES, WINDOW], U32, name="tok_words", align_bytes=64)
+        tok_scales = keep.tile([P, 3, WINDOW], U8, name="tok_scales", align_bytes=64)
+        slot_words = [keep.tile([P, S], U32, name="slot_words%d" % s, align_bytes=64) for s in range(PASSES)]
+        slot_scales = [keep.tile([P, S], U8, name="slot_scales%d" % g, align_bytes=64) for g in range(3)]
+        zeros = keep.tile([P, PAD], F32, name="zeros")
+        y = keep.tile([P, S + PAD], F32, name="y")
+        prod = [keep.tile([P, T], F32, name="prod%d" % r) for r in range(TOP)]
+        part = keep.tile([P, T], F32, name="part")
+        total = keep.tile([P, T], F32, name="total")
+        acc = [psum.tile([P, C], F32, name="acc%d" % e) for e in range(E)]
+
+        nc.vector.memset(w4_sc[:].rearrange("p a n -> p (a n)").bitcast(I32), 0)
+        nc.vector.memset(w8_sc[:].rearrange("p a n -> p (a n)").bitcast(I32), 0)
+        nc.vector.memset(zeros[:], 0.0)
+        nc.vector.memset(tok_scales[:].rearrange("p g t -> p (g t)").bitcast(I32), 0)
+        nc.vector.memset(tok_words[:, :, T:WINDOW].bitcast(I32), 0)
+        nc.scalar.activation(y[:, S : S + PAD], zeros[:], GELU)
+
+        for sc_sb, sc in ((w4_sc, w4_scales), (w8_sc, w8_scales)):
+            for r in range(4):
+                nc.gpsimd.dma_start(
+                    sc_sb[r:P:32, :, :].bitcast(I32),
+                    sc[:, :, r:16:4, :].rearrange("e a q n -> q (e a) n").bitcast(I32),
+                )
+
+        small = [(offs_sb, offs), (bias, b), (pos_sb[0], pos1), (pos_sb[1], pos2), (pos_sb[2], pos3)]
+        for s, (fmt, a, g, row) in enumerate(ORDER):
+            k0 = 512 * a + (K8 if fmt == "e2m1" else 0)
+            for c in range(CHUNKS):
+                nc.sync.dma_start(
+                    raw[s][c][:],
+                    xT[k0 : k0 + 512, c * CHUNK : (c + 1) * CHUNK].rearrange("(p j) t -> p j t", j=4),
+                )
+            nc.sync.dma_start(small[s][0][:], small[s][1])
+        for a in range(PASSES4):
+            nc.sync.dma_start(w4_sb[a][:].bitcast(I32), w4_words[:, a, :, :].rearrange("e p b -> p e b").bitcast(I32))
+        for a in range(PASSES8):
+            nc.sync.dma_start(
+                w8_sb[a][:].bitcast(I32), w8_words[:, a, :, :, :].rearrange("e p n r -> p e (n r)").bitcast(I32)
+            )
+        for r in range(TOP):
+            nc.sync.dma_start(gate_sb[r][:], gate[r, :, :])
+
+        def interleave(engine_copy, s, c, t0, t1):
+            engine_copy(
+                grouped[s][c][:, t0:t1, :].rearrange("p (c i) j -> p c j i", i=4),
+                raw[s][c][:, :, t0:t1].rearrange("p j (c i) -> p c j i", i=4),
+            )
+
+        def quantise(s, c):
+            fmt, a, g, row = ORDER[s]
+            cols = slice(c * CHUNK, (c + 1) * CHUNK)
+            nc.vector.quantize_mx(
+                out=tok_words[:, s, cols].bitcast(FP8X4),
+                scales=tok_scales[row:P, g, cols],
+                in_=grouped[s][c][:].rearrange("p t j -> p (t j)"),
+            )
+
+        def gather_words(s, e0, e1):
+            nc.vector.tensor_copy(
+                slot_words[s][:, e0 * C : e1 * C], tok_words[:, s, :].indirect(offs_sb[:, e0 * C // 16 : e1 * C // 16])
+            )
+
+        def gather_scales(g, e0, e1):
+            nc.vector.tensor_copy(
+                slot_scales[g][:, e0 * C : e1 * C], tok_scales[:, g, :].indirect(offs_sb[:, e0 * C // 16 : e1 * C // 16])
+            )
+
+        def multiply(s, e):
+            fmt, a, g, row = ORDER[s]
+            slots = slice(e * C, (e + 1) * C)
+            if fmt == "e2m1":
+                w, w_scale = w4_sb[a][:, e, :].bitcast(FP4X4), w4_sc[:, e * PASSES4 + a, :]
+            else:
+                w, w_scale = w8_sb[a][:, e, :].bitcast(FP8X4), w8_sc[:, e * PASSES8 + a, :]
+            nc.tensor.matmul_mx(
+                out=acc[e][:],
+                lhsT=w,
+                lhsT_scale=w_scale,
+                rhs=slot_words[s][:, slots].bitcast(FP8X4),
+                rhs_scale=slot_scales[g][row:P, slots],
+                start=(s == 0),
+                stop=(s == PASSES - 1),
+            )
+
+        for s in range(PASSES):
+            for c in range(CHUNKS):
+                if (s, c) == (0, 2):
+                    interleave(nc.scalar.copy, s, c, 0, 80)
+                    interleave(nc.vector.tensor_copy, s, c, 80, CHUNK)
+                elif (s, c) in ((0, 1), (PASSES - 1, 2)):
+                    interleave(nc.vector.tensor_copy, s, c, 0, CHUNK)
+                else:
+                    interleave(nc.scalar.copy, s, c, 0, CHUNK)
+                quantise(s, c)
+            if s < PASSES - 1:
+                gather_words(s, 0, E)
+            if s < 2:
+                gather_scales(s, 0, E)
+                for e in range(E):
+                    multiply(s, e)
+        for e0, e1 in LAST_GROUPS:
+            gather_scales(2, e0, e1)
+            gather_words(PASSES - 1, e0, e1)
+            for s in range(2, PASSES):
+                for e in range(e0, e1):
+                    multiply(s, e)
+            for e in range(e0, e1):
+                nc.scalar.activation(y[:, e * C : (e + 1) * C], acc[e][:], GELU, bias=bias[:, e : e + 1])
+
+        def weigh(r, t0, t1):
+            nc.vector.tensor_tensor(
+                prod[r][:, t0:t1], y[:].indirect(pos_sb[r][:, t0 // 16 : t1 // 16]), gate_sb[r][:, t0:t1], MULT
+            )
+
+        def add(dst, u, v, t0, t1):
+            nc.vector.tensor_tensor(dst[:, t0:t1], u[:, t0:t1], v[:, t0:t1], ADD)
+
+        (a0, a1), (b0, b1) = OUT_PARTS
+        weigh(0, a0, a1)
+        weigh(1, a0, a1)
+        weigh(2, a0, a1)
+        add(part, prod[0], prod[1], a0, a1)
+        weigh(0, b0, b1)
+        add(total, part, prod[2], a0, a1)
+        nc.sync.dma_start(out[:, a0:a1], total[:, a0:a1])
+        weigh(1, b0, b1)
+        weigh(2, b0, b1)
+        add(part, prod[0], prod[1], b0, b1)
+        add(total, part, prod[2], b0, b1)
+        nc.sync.dma_start(out[:, b0:b1], total[:, b0:b1])

@@ -22,8 +22,10 @@ ADD = mybir.AluOpType.add
 P = 128
 PASSES8, PASSES4 = 2, 3
 PASSES = 5
-CHUNK = 256
-CHUNKS = T // CHUNK
+EDGE_LOADS = [(0, 256), (256, 512), (512, 640), (640, 768)]
+MID_LOADS = [(0, 256), (256, 512), (512, 768)]
+LOADS = [EDGE_LOADS, MID_LOADS, MID_LOADS, MID_LOADS, EDGE_LOADS]
+ON_VECTOR = [(0, 1), (0, 3)]
 WINDOW = 1024
 ORDER = [("e2m1", 0, 0, 0), ("e2m1", 1, 1, 0), ("e2m1", 2, 2, 0), ("e4m3", 0, 2, 4), ("e4m3", 1, 2, 8)]
 LAST_GROUPS = [(0, 3), (3, 5), (5, 6)]
@@ -46,8 +48,10 @@ def tile_moe_ecr_lin_gelu_kernel(
         w4_sb = [keep.tile([P, E, 2 * N], U8, name="w4_sb%d" % a, align_bytes=64) for a in range(PASSES4)]
         w8_sc = keep.tile([P, E * PASSES8, N], U8, name="w8_sc", align_bytes=64)
         w4_sc = keep.tile([P, E * PASSES4, N], U8, name="w4_sc", align_bytes=64)
-        raw = [[keep.tile([P, 4, CHUNK], F32, name="raw%d_%d" % (s, c)) for c in range(CHUNKS)] for s in range(PASSES)]
-        grouped = [[keep.tile([P, CHUNK, 4], BF16, name="grouped%d_%d" % (s, c), align_bytes=64) for c in range(CHUNKS)] for s in range(PASSES)]
+        raw = [
+            [keep.tile([P, 4, t1 - t0], F32, name="raw%d_%d" % (s, t0)) for t0, t1 in LOADS[s]] for s in range(PASSES)
+        ]
+        grouped = [keep.tile([P, T, 4], BF16, name="grouped%d" % s, align_bytes=64) for s in range(PASSES)]
         tok_words = keep.tile([P, PASSES, WINDOW], U32, name="tok_words", align_bytes=64)
         tok_scales = keep.tile([P, 3, WINDOW], U8, name="tok_scales", align_bytes=64)
         slot_words = [keep.tile([P, S], U32, name="slot_words%d" % s, align_bytes=64) for s in range(PASSES)]
@@ -66,44 +70,51 @@ def tile_moe_ecr_lin_gelu_kernel(
         nc.vector.memset(tok_words[:, :, T:WINDOW].bitcast(I32), 0)
         nc.scalar.activation(y[:, S : S + PAD], zeros[:], GELU)
 
-        for sc_sb, sc in ((w4_sc, w4_scales), (w8_sc, w8_scales)):
+        for s, (fmt, a, g, row) in enumerate(ORDER):
+            k0 = 512 * a + (K8 if fmt == "e2m1" else 0)
+            for c, (t0, t1) in enumerate(LOADS[s]):
+                nc.sync.dma_start(raw[s][c][:], xT[k0 : k0 + 512, t0:t1].rearrange("(p j) t -> p j t", j=4))
+            if s == 0:
+                nc.sync.dma_start(offs_sb[:], offs)
+
+        def load_scales(sc_sb, sc):
             for r in range(4):
-                nc.gpsimd.dma_start(
+                nc.sync.dma_start(
                     sc_sb[r:P:32, :, :].bitcast(I32),
                     sc[:, :, r:16:4, :].rearrange("e a q n -> q (e a) n").bitcast(I32),
                 )
 
-        small = [(offs_sb, offs), (bias, b), (pos_sb[0], pos1), (pos_sb[1], pos2), (pos_sb[2], pos3)]
-        for s, (fmt, a, g, row) in enumerate(ORDER):
-            k0 = 512 * a + (K8 if fmt == "e2m1" else 0)
-            for c in range(CHUNKS):
-                nc.sync.dma_start(
-                    raw[s][c][:],
-                    xT[k0 : k0 + 512, c * CHUNK : (c + 1) * CHUNK].rearrange("(p j) t -> p j t", j=4),
-                )
-            nc.sync.dma_start(small[s][0][:], small[s][1])
-        for a in range(PASSES4):
+        def load_w4(a):
             nc.sync.dma_start(w4_sb[a][:].bitcast(I32), w4_words[:, a, :, :].rearrange("e p b -> p e b").bitcast(I32))
+
+        load_scales(w4_sc, w4_scales)
+        load_w4(0)
+        load_w4(1)
+        load_scales(w8_sc, w8_scales)
+        load_w4(2)
+        nc.sync.dma_start(bias[:], b)
         for a in range(PASSES8):
             nc.sync.dma_start(
                 w8_sb[a][:].bitcast(I32), w8_words[:, a, :, :, :].rearrange("e p n r -> p e (n r)").bitcast(I32)
             )
-        for r in range(TOP):
+        for r, pos in enumerate((pos1, pos2, pos3)):
+            nc.sync.dma_start(pos_sb[r][:], pos)
             nc.sync.dma_start(gate_sb[r][:], gate[r, :, :])
 
-        def interleave(engine_copy, s, c, t0, t1):
-            engine_copy(
-                grouped[s][c][:, t0:t1, :].rearrange("p (c i) j -> p c j i", i=4),
-                raw[s][c][:, :, t0:t1].rearrange("p j (c i) -> p c j i", i=4),
+        def interleave(s, c):
+            t0, t1 = LOADS[s][c]
+            copy = nc.vector.tensor_copy if (s, c) in ON_VECTOR else nc.scalar.copy
+            copy(
+                grouped[s][:, t0:t1, :].rearrange("p (c i) j -> p c j i", i=4),
+                raw[s][c][:].rearrange("p j (c i) -> p c j i", i=4),
             )
 
-        def quantise(s, c):
+        def quantise(s, t0, t1):
             fmt, a, g, row = ORDER[s]
-            cols = slice(c * CHUNK, (c + 1) * CHUNK)
             nc.vector.quantize_mx(
-                out=tok_words[:, s, cols].bitcast(FP8X4),
-                scales=tok_scales[row:P, g, cols],
-                in_=grouped[s][c][:].rearrange("p t j -> p (t j)"),
+                out=tok_words[:, s, t0:t1].bitcast(FP8X4),
+                scales=tok_scales[row:P, g, t0:t1],
+                in_=grouped[s][:, t0:t1, :].rearrange("p t j -> p (t j)"),
             )
 
         def gather_words(s, e0, e1):
@@ -133,22 +144,30 @@ def tile_moe_ecr_lin_gelu_kernel(
                 stop=(s == PASSES - 1),
             )
 
-        for s in range(PASSES):
-            for c in range(CHUNKS):
-                if (s, c) == (0, 2):
-                    interleave(nc.scalar.copy, s, c, 0, 80)
-                    interleave(nc.vector.tensor_copy, s, c, 80, CHUNK)
-                elif (s, c) in ((0, 1), (PASSES - 1, 2)):
-                    interleave(nc.vector.tensor_copy, s, c, 0, CHUNK)
-                else:
-                    interleave(nc.scalar.copy, s, c, 0, CHUNK)
-                quantise(s, c)
-            if s < PASSES - 1:
-                gather_words(s, 0, E)
-            if s < 2:
-                gather_scales(s, 0, E)
-                for e in range(E):
-                    multiply(s, e)
+        def supply(s):
+            for c in range(len(LOADS[s])):
+                interleave(s, c)
+            quantise(s, 0, 512)
+            for t0, t1 in LOADS[s][2:]:
+                quantise(s, t0, t1)
+
+        half = E // 2
+        supply(0)
+        gather_words(0, 0, E)
+        supply(1)
+        gather_scales(0, 0, E)
+        gather_words(1, 0, E)
+        supply(2)
+        gather_scales(1, 0, E)
+        gather_words(2, 0, half)
+        supply(3)
+        gather_words(2, half, E)
+        gather_words(3, 0, half)
+        supply(4)
+        gather_words(3, half, E)
+        for s in range(2):
+            for e in range(E):
+                multiply(s, e)
         for e0, e1 in LAST_GROUPS:
             gather_scales(2, e0, e1)
             gather_words(PASSES - 1, e0, e1)
@@ -169,13 +188,13 @@ def tile_moe_ecr_lin_gelu_kernel(
         (a0, a1), (b0, b1) = OUT_PARTS
         weigh(0, a0, a1)
         weigh(1, a0, a1)
-        weigh(2, a0, a1)
-        add(part, prod[0], prod[1], a0, a1)
         weigh(0, b0, b1)
+        add(part, prod[0], prod[1], a0, a1)
+        weigh(1, b0, b1)
+        weigh(2, a0, a1)
+        add(part, prod[0], prod[1], b0, b1)
+        weigh(2, b0, b1)
         add(total, part, prod[2], a0, a1)
         nc.sync.dma_start(out[:, a0:a1], total[:, a0:a1])
-        weigh(1, b0, b1)
-        weigh(2, b0, b1)
-        add(part, prod[0], prod[1], b0, b1)
         add(total, part, prod[2], b0, b1)
-        nc.sync.dma_start(out[:, b0:b1], total[:, b0:b1])
+        nc.scalar.dma_start(out[:, b0:b1], total[:, b0:b1])

@@ -27,7 +27,7 @@ MID_LOADS = [(0, 256), (256, 512), (512, 768)]
 LOADS = [EDGE_LOADS, MID_LOADS, MID_LOADS, MID_LOADS, EDGE_LOADS]
 ON_VECTOR = [(0, 1), (0, 3)]
 WINDOW = 1024
-ORDER = [("e2m1", 0, 0, 0), ("e2m1", 1, 1, 0), ("e2m1", 2, 2, 0), ("e4m3", 0, 2, 4), ("e4m3", 1, 2, 8)]
+ORDER = [("e2m1", 0, 0, 0), ("e2m1", 1, 1, 0), ("e4m3", 0, 1, 4), ("e2m1", 2, 2, 0), ("e4m3", 1, 2, 4)]
 LAST_GROUPS = [(0, 3), (3, 5), (5, 6)]
 OUT_PARTS = [(0, 512), (512, 768)]
 
@@ -43,7 +43,7 @@ def tile_moe_ecr_lin_gelu_kernel(
         offs_sb = keep.tile([P, S // 16], U16, name="offs_sb")
         pos_sb = [keep.tile([P, T // 16], U16, name="pos_sb%d" % r) for r in range(TOP)]
         bias = keep.tile([P, E], F32, name="bias")
-        gate_sb = [keep.tile([P, T], F32, name="gate_sb%d" % r) for r in range(TOP)]
+        gate_sb = keep.tile([P, TOP, T], F32, name="gate_sb")
         w8_sb = [keep.tile([P, E, 4 * N], U8, name="w8_sb%d" % a, align_bytes=64) for a in range(PASSES8)]
         w4_sb = [keep.tile([P, E, 2 * N], U8, name="w4_sb%d" % a, align_bytes=64) for a in range(PASSES4)]
         w8_sc = keep.tile([P, E * PASSES8, N], U8, name="w8_sc", align_bytes=64)
@@ -91,15 +91,23 @@ def tile_moe_ecr_lin_gelu_kernel(
         load_w4(0)
         load_w4(1)
         load_scales(w8_sc, w8_scales)
+
+        def load_w8(a, e0, e1):
+            nc.sync.dma_start(
+                w8_sb[a][:, e0:e1, :].bitcast(I32),
+                w8_words[e0:e1, a, :, :, :].rearrange("e p n r -> p e (n r)").bitcast(I32),
+            )
+
+        load_w8(0, 0, E)
         load_w4(2)
         nc.sync.dma_start(bias[:], b)
-        for a in range(PASSES8):
-            nc.sync.dma_start(
-                w8_sb[a][:].bitcast(I32), w8_words[:, a, :, :, :].rearrange("e p n r -> p e (n r)").bitcast(I32)
-            )
+        for e0, e1 in LAST_GROUPS:
+            load_w8(1, e0, e1)
+        (a0, a1), (b0, b1) = OUT_PARTS
         for r, pos in enumerate((pos1, pos2, pos3)):
             nc.sync.dma_start(pos_sb[r][:], pos)
-            nc.sync.dma_start(gate_sb[r][:], gate[r, :, :])
+            nc.sync.dma_start(gate_sb[:, r, a0:a1], gate[r, :, a0:a1])
+        nc.sync.dma_start(gate_sb[:, :, b0:b1], gate[:, :, b0:b1].rearrange("r n t -> n r t"))
 
         def interleave(s, c):
             t0, t1 = LOADS[s][c]
@@ -119,7 +127,8 @@ def tile_moe_ecr_lin_gelu_kernel(
 
         def gather_words(s, e0, e1):
             nc.vector.tensor_copy(
-                slot_words[s][:, e0 * C : e1 * C], tok_words[:, s, :].indirect(offs_sb[:, e0 * C // 16 : e1 * C // 16])
+                slot_words[s][:, e0 * C : e1 * C],
+                tok_words[:, s, :].indirect(offs_sb[:, e0 * C // 16 : e1 * C // 16]),
             )
 
         def gather_scales(g, e0, e1):
@@ -156,22 +165,22 @@ def tile_moe_ecr_lin_gelu_kernel(
         gather_words(0, 0, E)
         supply(1)
         gather_scales(0, 0, E)
-        gather_words(1, 0, E)
+        gather_words(1, 0, half)
         supply(2)
-        gather_scales(1, 0, E)
-        gather_words(2, 0, half)
+        gather_words(1, half, E)
+        gather_words(2, 0, E)
         supply(3)
-        gather_words(2, half, E)
+        gather_scales(1, 0, E)
         gather_words(3, 0, half)
         supply(4)
         gather_words(3, half, E)
-        for s in range(2):
+        for s in range(3):
             for e in range(E):
                 multiply(s, e)
         for e0, e1 in LAST_GROUPS:
             gather_scales(2, e0, e1)
             gather_words(PASSES - 1, e0, e1)
-            for s in range(2, PASSES):
+            for s in range(3, PASSES):
                 for e in range(e0, e1):
                     multiply(s, e)
             for e in range(e0, e1):
@@ -179,22 +188,24 @@ def tile_moe_ecr_lin_gelu_kernel(
 
         def weigh(r, t0, t1):
             nc.vector.tensor_tensor(
-                prod[r][:, t0:t1], y[:].indirect(pos_sb[r][:, t0 // 16 : t1 // 16]), gate_sb[r][:, t0:t1], MULT
+                prod[r][:, t0:t1], y[:].indirect(pos_sb[r][:, t0 // 16 : t1 // 16]), gate_sb[:, r, t0:t1], MULT
             )
 
         def add(dst, u, v, t0, t1):
             nc.vector.tensor_tensor(dst[:, t0:t1], u[:, t0:t1], v[:, t0:t1], ADD)
 
-        (a0, a1), (b0, b1) = OUT_PARTS
+        bm = (b0 + b1) // 2
         weigh(0, a0, a1)
         weigh(1, a0, a1)
-        weigh(0, b0, b1)
-        add(part, prod[0], prod[1], a0, a1)
-        weigh(1, b0, b1)
         weigh(2, a0, a1)
-        add(part, prod[0], prod[1], b0, b1)
-        weigh(2, b0, b1)
+        add(part, prod[0], prod[1], a0, a1)
+        weigh(0, b0, b1)
         add(total, part, prod[2], a0, a1)
         nc.sync.dma_start(out[:, a0:a1], total[:, a0:a1])
-        add(total, part, prod[2], b0, b1)
+        weigh(1, b0, b1)
+        weigh(2, b0, b1)
+        add(part, prod[0], prod[1], b0, bm)
+        add(part, prod[0], prod[1], bm, b1)
+        add(total, part, prod[2], b0, bm)
+        add(total, part, prod[2], bm, b1)
         nc.scalar.dma_start(out[:, b0:b1], total[:, b0:b1])

@@ -1,6 +1,7 @@
 from contextlib import ExitStack
 
 import concourse.mybir as mybir
+from concourse.masks import make_identity
 
 K, T, E, C, N = 2560, 768, 6, 128, 128
 TOP, PAD, K8 = 3, 64, 1024
@@ -30,6 +31,7 @@ WINDOW = 1024
 ORDER = [("e2m1", 0, 0, 0), ("e2m1", 1, 1, 0), ("e4m3", 0, 1, 4), ("e2m1", 2, 2, 0), ("e4m3", 1, 2, 4)]
 LAST_GROUPS = [(0, 3), (3, 5), (5, 6)]
 OUT_PARTS = [(0, 512), (512, 768)]
+TURNED = [(0, 256), (256, 512)]
 
 
 def tile_moe_ecr_lin_gelu_kernel(
@@ -61,7 +63,15 @@ def tile_moe_ecr_lin_gelu_kernel(
         prod = [keep.tile([P, T], F32, name="prod%d" % r) for r in range(TOP)]
         part = keep.tile([P, T], F32, name="part")
         total = keep.tile([P, T], F32, name="total")
-        acc = [psum.tile([P, C], F32, name="acc%d" % e) for e in range(E)]
+        ident = keep.tile([P, P], F32, name="ident")
+        turned = [keep.tile([P, t1 - t0], F32, name="turned%d" % t0) for t0, t1 in TURNED]
+        sums = [keep.tile([P, t1 - t0], F32, name="sums%d" % t0) for t0, t1 in TURNED]
+
+        def bank(i, name):
+            return psum.tile([P, 4 * P], F32, name=name, tag="bank%d" % i)
+
+        acc = [bank(e, "acc%d" % e)[:, 0:C] for e in range(E)]
+        make_identity(nc, ident[:])
 
         nc.vector.memset(w4_sc[:].rearrange("p a n -> p (a n)").bitcast(I32), 0)
         nc.vector.memset(w8_sc[:].rearrange("p a n -> p (a n)").bitcast(I32), 0)
@@ -144,7 +154,7 @@ def tile_moe_ecr_lin_gelu_kernel(
             else:
                 w, w_scale = w8_sb[a][:, e, :].bitcast(FP8X4), w8_sc[:, e * PASSES8 + a, :]
             nc.tensor.matmul_mx(
-                out=acc[e][:],
+                out=acc[e],
                 lhsT=w,
                 lhsT_scale=w_scale,
                 rhs=slot_words[s][:, slots].bitcast(FP8X4),
@@ -184,7 +194,7 @@ def tile_moe_ecr_lin_gelu_kernel(
                 for e in range(e0, e1):
                     multiply(s, e)
             for e in range(e0, e1):
-                nc.scalar.activation(y[:, e * C : (e + 1) * C], acc[e][:], GELU, bias=bias[:, e : e + 1])
+                nc.scalar.activation(y[:, e * C : (e + 1) * C], acc[e], GELU, bias=bias[:, e : e + 1])
 
         def weigh(r, t0, t1):
             nc.vector.tensor_tensor(
@@ -194,18 +204,40 @@ def tile_moe_ecr_lin_gelu_kernel(
         def add(dst, u, v, t0, t1):
             nc.vector.tensor_tensor(dst[:, t0:t1], u[:, t0:t1], v[:, t0:t1], ADD)
 
+        def weigh_and_turn(i):
+            t0, t1 = TURNED[i]
+            ps = bank(6 + i, "turn_ps%d" % i)
+            blocks = range(t0, t1, P)
+            for r in range(TOP):
+                weigh(r, t0, t1)
+                for t in blocks:
+                    nc.tensor.matmul(
+                        ps[:, t - t0 : t - t0 + P],
+                        lhsT=prod[r][:, t : t + P],
+                        rhs=ident[:],
+                        is_transpose=True,
+                        start=(r == 0 and t == t0),
+                        stop=(r == TOP - 1 and t == t1 - P),
+                    )
+            nc.scalar.copy(turned[i][:], ps[:, 0 : t1 - t0])
+
+        def turn_back(i):
+            t0, t1 = TURNED[i]
+            ps = bank(i, "back_ps%d" % i)
+            for t in range(0, t1 - t0, P):
+                nc.tensor.transpose(ps[:, t : t + P], turned[i][:, t : t + P], ident[:])
+            nc.scalar.copy(sums[i][:], ps[:, 0 : t1 - t0])
+            nc.scalar.dma_start(out[:, t0:t1], sums[i][:])
+
         bm = (b0 + b1) // 2
-        weigh(0, a0, a1)
-        weigh(1, a0, a1)
-        weigh(2, a0, a1)
-        add(part, prod[0], prod[1], a0, a1)
-        weigh(0, b0, b1)
-        add(total, part, prod[2], a0, a1)
-        nc.sync.dma_start(out[:, a0:a1], total[:, a0:a1])
-        weigh(1, b0, b1)
-        weigh(2, b0, b1)
+        weigh_and_turn(0)
+        weigh_and_turn(1)
+        turn_back(0)
+        turn_back(1)
+        for r in range(TOP):
+            weigh(r, b0, b1)
         add(part, prod[0], prod[1], b0, bm)
         add(part, prod[0], prod[1], bm, b1)
         add(total, part, prod[2], b0, bm)
         add(total, part, prod[2], bm, b1)
-        nc.scalar.dma_start(out[:, b0:b1], total[:, b0:b1])
+        nc.sync.dma_start(out[:, b0:b1], total[:, b0:b1])

@@ -26,12 +26,16 @@ PASSES = 5
 EDGE_LOADS = [(0, 256), (256, 512), (512, 640), (640, 768)]
 MID_LOADS = [(0, 256), (256, 512), (512, 768)]
 LOADS = [EDGE_LOADS, MID_LOADS, MID_LOADS, MID_LOADS, EDGE_LOADS]
-ON_VECTOR = [(0, 1), (0, 3)]
+FIRST_COPIES = [(0, 256), (256, 384), (384, 512), (512, 640), (640, 768)]
+COPIES = [FIRST_COPIES] + LOADS[1:]
+ON_VECTOR = [(0, 1), (0, 4)]
+FIRST_QUANTISE = EDGE_LOADS
+QUANTISE = [FIRST_QUANTISE] + [[(0, 512)] + loads[2:] for loads in LOADS[1:]]
 WINDOW = 1024
 ORDER = [("e2m1", 0, 0, 0), ("e2m1", 1, 1, 0), ("e4m3", 0, 1, 4), ("e2m1", 2, 2, 0), ("e4m3", 1, 2, 4)]
 LAST_GROUPS = [(0, 3), (3, 5), (5, 6)]
-OUT_PARTS = [(0, 512), (512, 768)]
-TURNED = [(0, 256), (256, 512)]
+OUT_PARTS = [(0, 384), (384, 768)]
+TURNED = [(0, 256), (256, 384)]
 
 
 def tile_moe_ecr_lin_gelu_kernel(
@@ -87,20 +91,20 @@ def tile_moe_ecr_lin_gelu_kernel(
             if s == 0:
                 nc.sync.dma_start(offs_sb[:], offs)
 
-        def load_scales(sc_sb, sc):
-            for r in range(4):
-                nc.sync.dma_start(
-                    sc_sb[r:P:32, :, :].bitcast(I32),
-                    sc[:, :, r:16:4, :].rearrange("e a q n -> q (e a) n").bitcast(I32),
-                )
+        def load_scales(sc_sb, sc, row, r):
+            nc.sync.dma_start(
+                sc_sb[row + r : P : 32, :, :].bitcast(I32),
+                sc[:, :, r:16:4, :].rearrange("e a q n -> q (e a) n").bitcast(I32),
+            )
 
         def load_w4(a):
             nc.sync.dma_start(w4_sb[a][:].bitcast(I32), w4_words[:, a, :, :].rearrange("e p b -> p e b").bitcast(I32))
 
-        load_scales(w4_sc, w4_scales)
+        for r in range(4):
+            load_scales(w4_sc, w4_scales, 0, r)
+            load_scales(w8_sc, w8_scales, 4, r)
         load_w4(0)
         load_w4(1)
-        load_scales(w8_sc, w8_scales)
 
         def load_w8(a, e0, e1):
             nc.sync.dma_start(
@@ -114,17 +118,21 @@ def tile_moe_ecr_lin_gelu_kernel(
         for e0, e1 in LAST_GROUPS:
             load_w8(1, e0, e1)
         (a0, a1), (b0, b1) = OUT_PARTS
+        f0, f1 = TURNED[0]
         for r, pos in enumerate((pos1, pos2, pos3)):
             nc.sync.dma_start(pos_sb[r][:], pos)
-            nc.sync.dma_start(gate_sb[:, r, a0:a1], gate[r, :, a0:a1])
-        nc.sync.dma_start(gate_sb[:, :, b0:b1], gate[:, :, b0:b1].rearrange("r n t -> n r t"))
+            nc.sync.dma_start(gate_sb[:, r, f0:f1], gate[r, :, f0:f1])
+        for t0, t1 in TURNED[1:] + [(b0, b1)]:
+            nc.sync.dma_start(gate_sb[:, :, t0:t1], gate[:, :, t0:t1].rearrange("r n t -> n r t"))
 
         def interleave(s, c):
-            t0, t1 = LOADS[s][c]
+            t0, t1 = COPIES[s][c]
+            load = max(i for i, (u0, u1) in enumerate(LOADS[s]) if u0 <= t0)
+            u0 = LOADS[s][load][0]
             copy = nc.vector.tensor_copy if (s, c) in ON_VECTOR else nc.scalar.copy
             copy(
                 grouped[s][:, t0:t1, :].rearrange("p (c i) j -> p c j i", i=4),
-                raw[s][c][:].rearrange("p j (c i) -> p c j i", i=4),
+                raw[s][load][:, :, t0 - u0 : t1 - u0].rearrange("p j (c i) -> p c j i", i=4),
             )
 
         def quantise(s, t0, t1):
@@ -152,7 +160,7 @@ def tile_moe_ecr_lin_gelu_kernel(
             if fmt == "e2m1":
                 w, w_scale = w4_sb[a][:, e, :].bitcast(FP4X4), w4_sc[:, e * PASSES4 + a, :]
             else:
-                w, w_scale = w8_sb[a][:, e, :].bitcast(FP8X4), w8_sc[:, e * PASSES8 + a, :]
+                w, w_scale = w8_sb[a][:, e, :].bitcast(FP8X4), w8_sc[4:P, e * PASSES8 + a, :]
             nc.tensor.matmul_mx(
                 out=acc[e],
                 lhsT=w,
@@ -164,10 +172,9 @@ def tile_moe_ecr_lin_gelu_kernel(
             )
 
         def supply(s):
-            for c in range(len(LOADS[s])):
+            for c in range(len(COPIES[s])):
                 interleave(s, c)
-            quantise(s, 0, 512)
-            for t0, t1 in LOADS[s][2:]:
+            for t0, t1 in QUANTISE[s]:
                 quantise(s, t0, t1)
 
         half = E // 2
@@ -227,17 +234,18 @@ def tile_moe_ecr_lin_gelu_kernel(
             for t in range(0, t1 - t0, P):
                 nc.tensor.transpose(ps[:, t : t + P], turned[i][:, t : t + P], ident[:])
             nc.scalar.copy(sums[i][:], ps[:, 0 : t1 - t0])
-            nc.scalar.dma_start(out[:, t0:t1], sums[i][:])
+            queue = nc.scalar if i == len(TURNED) - 1 else nc.sync
+            queue.dma_start(out[:, t0:t1], sums[i][:])
 
         bm = (b0 + b1) // 2
         weigh_and_turn(0)
-        weigh_and_turn(1)
         turn_back(0)
+        weigh_and_turn(1)
         turn_back(1)
         for r in range(TOP):
             weigh(r, b0, b1)
         add(part, prod[0], prod[1], b0, bm)
         add(part, prod[0], prod[1], bm, b1)
-        add(total, part, prod[2], b0, bm)
-        add(total, part, prod[2], bm, b1)
-        nc.sync.dma_start(out[:, b0:b1], total[:, b0:b1])
+        for t0, t1 in ((b0, bm), (bm, b1)):
+            add(total, part, prod[2], t0, t1)
+            nc.sync.dma_start(out[:, t0:t1], total[:, t0:t1])

@@ -28,7 +28,7 @@ MID_LOADS = [(0, 256), (256, 512), (512, 768)]
 LOADS = [EDGE_LOADS, MID_LOADS, MID_LOADS, MID_LOADS, EDGE_LOADS]
 FIRST_COPIES = [(0, 256), (256, 384), (384, 512), (512, 640), (640, 768)]
 COPIES = [FIRST_COPIES] + LOADS[1:]
-ON_VECTOR = [(0, 1), (0, 4)]
+ON_VECTOR = [(0, 1), (0, 4), (4, 3)]
 FIRST_QUANTISE = EDGE_LOADS
 QUANTISE = [FIRST_QUANTISE] + [[(0, 512)] + loads[2:] for loads in LOADS[1:]]
 WINDOW = 1024
@@ -102,9 +102,10 @@ def tile_moe_ecr_lin_gelu_kernel(
 
         for r in range(4):
             load_scales(w4_sc, w4_scales, 0, r)
-            load_scales(w8_sc, w8_scales, 4, r)
         load_w4(0)
         load_w4(1)
+        for r in range(4):
+            load_scales(w8_sc, w8_scales, 4, r)
 
         def load_w8(a, e0, e1):
             nc.sync.dma_start(

@@ -21,21 +21,31 @@ MULT = mybir.AluOpType.mult
 ADD = mybir.AluOpType.add
 
 P = 128
-PASSES8, PASSES4 = 2, 3
-PASSES = 5
+PACK = 4
+K_PASS = P * PACK
+PER_COLUMN = 16
+QUADRANT = 32
+PASSES8, PASSES4 = K8 // K_PASS, (K - K8) // K_PASS
+PASSES = PASSES8 + PASSES4
+
+ORDER = [("e2m1", 0, 0, 0), ("e2m1", 1, 1, 0), ("e4m3", 0, 1, 4), ("e2m1", 2, 2, 0), ("e4m3", 1, 2, 4)]
+SCALE_TILES = PASSES4
+W8_ROW = 4
+
 EDGE_LOADS = [(0, 256), (256, 512), (512, 640), (640, 768)]
 MID_LOADS = [(0, 256), (256, 512), (512, 768)]
 LOADS = [EDGE_LOADS, MID_LOADS, MID_LOADS, MID_LOADS, EDGE_LOADS]
 FIRST_COPIES = [(0, 256), (256, 384), (384, 512), (512, 640), (640, 768)]
 COPIES = [FIRST_COPIES] + LOADS[1:]
-ON_VECTOR = [(0, 1), (0, 4), (4, 3)]
-FIRST_QUANTISE = EDGE_LOADS
-QUANTISE = [FIRST_QUANTISE] + [[(0, 512)] + loads[2:] for loads in LOADS[1:]]
+ON_VECTOR = [(0, 1), (0, 4)]
+QUANTISE = [EDGE_LOADS] + [[(0, 512)] + loads[2:] for loads in LOADS[1:]]
 WINDOW = 1024
-ORDER = [("e2m1", 0, 0, 0), ("e2m1", 1, 1, 0), ("e4m3", 0, 1, 4), ("e2m1", 2, 2, 0), ("e4m3", 1, 2, 4)]
-LAST_GROUPS = [(0, 3), (3, 5), (5, 6)]
-OUT_PARTS = [(0, 384), (384, 768)]
+
+HALF = E // 2
+LAST_GROUPS = [(0, HALF), (HALF, E - 1), (E - 1, E)]
+EARLY_PASSES = 2
 TURNED = [(0, 256), (256, 384)]
+ADDED = (384, T)
 
 
 def tile_moe_ecr_lin_gelu_kernel(
@@ -46,8 +56,8 @@ def tile_moe_ecr_lin_gelu_kernel(
         keep = ctx.enter_context(tc.tile_pool(name="keep", bufs=1))
         psum = ctx.enter_context(tc.psum_pool(name="psum", bufs=1))
 
-        offs_sb = keep.tile([P, S // 16], U16, name="offs_sb")
-        pos_sb = [keep.tile([P, T // 16], U16, name="pos_sb%d" % r) for r in range(TOP)]
+        offs_sb = keep.tile([P, S // PER_COLUMN], U16, name="offs_sb")
+        pos_sb = [keep.tile([P, T // PER_COLUMN], U16, name="pos_sb%d" % r) for r in range(TOP)]
         bias = keep.tile([P, E], F32, name="bias")
         gate_sb = keep.tile([P, TOP, T], F32, name="gate_sb")
         w8_sb = [keep.tile([P, E, 4 * N], U8, name="w8_sb%d" % a, align_bytes=64) for a in range(PASSES8)]
@@ -55,13 +65,14 @@ def tile_moe_ecr_lin_gelu_kernel(
         w8_sc = keep.tile([P, E * PASSES8, N], U8, name="w8_sc", align_bytes=64)
         w4_sc = keep.tile([P, E * PASSES4, N], U8, name="w4_sc", align_bytes=64)
         raw = [
-            [keep.tile([P, 4, t1 - t0], F32, name="raw%d_%d" % (s, t0)) for t0, t1 in LOADS[s]] for s in range(PASSES)
+            [keep.tile([P, PACK, t1 - t0], F32, name="raw%d_%d" % (s, t0)) for t0, t1 in LOADS[s]]
+            for s in range(PASSES)
         ]
-        grouped = [keep.tile([P, T, 4], BF16, name="grouped%d" % s, align_bytes=64) for s in range(PASSES)]
+        grouped = [keep.tile([P, T, PACK], BF16, name="grouped%d" % s, align_bytes=64) for s in range(PASSES)]
         tok_words = keep.tile([P, PASSES, WINDOW], U32, name="tok_words", align_bytes=64)
-        tok_scales = keep.tile([P, 3, WINDOW], U8, name="tok_scales", align_bytes=64)
+        tok_scales = keep.tile([P, SCALE_TILES, WINDOW], U8, name="tok_scales", align_bytes=64)
         slot_words = [keep.tile([P, S], U32, name="slot_words%d" % s, align_bytes=64) for s in range(PASSES)]
-        slot_scales = [keep.tile([P, S], U8, name="slot_scales%d" % g, align_bytes=64) for g in range(3)]
+        slot_scales = [keep.tile([P, S], U8, name="slot_scales%d" % g, align_bytes=64) for g in range(SCALE_TILES)]
         zeros = keep.tile([P, PAD], F32, name="zeros")
         y = keep.tile([P, S + PAD], F32, name="y")
         prod = [keep.tile([P, T], F32, name="prod%d" % r) for r in range(TOP)]
@@ -85,27 +96,21 @@ def tile_moe_ecr_lin_gelu_kernel(
         nc.scalar.activation(y[:, S : S + PAD], zeros[:], GELU)
 
         for s, (fmt, a, g, row) in enumerate(ORDER):
-            k0 = 512 * a + (K8 if fmt == "e2m1" else 0)
+            k0 = K_PASS * a + (K8 if fmt == "e2m1" else 0)
             for c, (t0, t1) in enumerate(LOADS[s]):
-                nc.sync.dma_start(raw[s][c][:], xT[k0 : k0 + 512, t0:t1].rearrange("(p j) t -> p j t", j=4))
+                nc.sync.dma_start(raw[s][c][:], xT[k0 : k0 + K_PASS, t0:t1].rearrange("(p j) t -> p j t", j=PACK))
             if s == 0:
                 nc.sync.dma_start(offs_sb[:], offs)
 
-        def load_scales(sc_sb, sc, row, r):
-            nc.sync.dma_start(
-                sc_sb[row + r : P : 32, :, :].bitcast(I32),
-                sc[:, :, r:16:4, :].rearrange("e a q n -> q (e a) n").bitcast(I32),
-            )
+        def load_scales(sc_sb, sc, row):
+            for r in range(4):
+                nc.sync.dma_start(
+                    sc_sb[row + r : P : QUADRANT, :, :].bitcast(I32),
+                    sc[:, :, r:16:4, :].rearrange("e a q n -> q (e a) n").bitcast(I32),
+                )
 
         def load_w4(a):
             nc.sync.dma_start(w4_sb[a][:].bitcast(I32), w4_words[:, a, :, :].rearrange("e p b -> p e b").bitcast(I32))
-
-        for r in range(4):
-            load_scales(w4_sc, w4_scales, 0, r)
-        load_w4(0)
-        load_w4(1)
-        for r in range(4):
-            load_scales(w8_sc, w8_scales, 4, r)
 
         def load_w8(a, e0, e1):
             nc.sync.dma_start(
@@ -113,27 +118,32 @@ def tile_moe_ecr_lin_gelu_kernel(
                 w8_words[e0:e1, a, :, :, :].rearrange("e p n r -> p e (n r)").bitcast(I32),
             )
 
-        load_w8(0, 0, E)
+        load_scales(w4_sc, w4_scales, 0)
+        load_w4(0)
+        load_w4(1)
+        load_scales(w8_sc, w8_scales, W8_ROW)
+        load_w8(0, 0, HALF)
         load_w4(2)
+        load_w8(1, 0, HALF)
         nc.sync.dma_start(bias[:], b)
-        for e0, e1 in LAST_GROUPS:
+        load_w8(0, HALF, E)
+        for e0, e1 in LAST_GROUPS[1:]:
             load_w8(1, e0, e1)
-        (a0, a1), (b0, b1) = OUT_PARTS
-        f0, f1 = TURNED[0]
+        first0, first1 = TURNED[0]
         for r, pos in enumerate((pos1, pos2, pos3)):
             nc.sync.dma_start(pos_sb[r][:], pos)
-            nc.sync.dma_start(gate_sb[:, r, f0:f1], gate[r, :, f0:f1])
-        for t0, t1 in TURNED[1:] + [(b0, b1)]:
+            nc.sync.dma_start(gate_sb[:, r, first0:first1], gate[r, :, first0:first1])
+        for t0, t1 in TURNED[1:] + [ADDED]:
             nc.sync.dma_start(gate_sb[:, :, t0:t1], gate[:, :, t0:t1].rearrange("r n t -> n r t"))
 
         def interleave(s, c):
             t0, t1 = COPIES[s][c]
             load = max(i for i, (u0, u1) in enumerate(LOADS[s]) if u0 <= t0)
-            u0 = LOADS[s][load][0]
+            base = LOADS[s][load][0]
             copy = nc.vector.tensor_copy if (s, c) in ON_VECTOR else nc.scalar.copy
             copy(
                 grouped[s][:, t0:t1, :].rearrange("p (c i) j -> p c j i", i=4),
-                raw[s][load][:, :, t0 - u0 : t1 - u0].rearrange("p j (c i) -> p c j i", i=4),
+                raw[s][load][:, :, t0 - base : t1 - base].rearrange("p j (c i) -> p c j i", i=4),
             )
 
         def quantise(s, t0, t1):
@@ -144,16 +154,20 @@ def tile_moe_ecr_lin_gelu_kernel(
                 in_=grouped[s][:, t0:t1, :].rearrange("p t j -> p (t j)"),
             )
 
+        def supply(s):
+            for c in range(len(COPIES[s])):
+                interleave(s, c)
+            for t0, t1 in QUANTISE[s]:
+                quantise(s, t0, t1)
+
+        def slot_entries(e0, e1):
+            return offs_sb[:, e0 * C // PER_COLUMN : e1 * C // PER_COLUMN]
+
         def gather_words(s, e0, e1):
-            nc.vector.tensor_copy(
-                slot_words[s][:, e0 * C : e1 * C],
-                tok_words[:, s, :].indirect(offs_sb[:, e0 * C // 16 : e1 * C // 16]),
-            )
+            nc.vector.tensor_copy(slot_words[s][:, e0 * C : e1 * C], tok_words[:, s, :].indirect(slot_entries(e0, e1)))
 
         def gather_scales(g, e0, e1):
-            nc.vector.tensor_copy(
-                slot_scales[g][:, e0 * C : e1 * C], tok_scales[:, g, :].indirect(offs_sb[:, e0 * C // 16 : e1 * C // 16])
-            )
+            nc.vector.tensor_copy(slot_scales[g][:, e0 * C : e1 * C], tok_scales[:, g, :].indirect(slot_entries(e0, e1)))
 
         def multiply(s, e):
             fmt, a, g, row = ORDER[s]
@@ -161,7 +175,7 @@ def tile_moe_ecr_lin_gelu_kernel(
             if fmt == "e2m1":
                 w, w_scale = w4_sb[a][:, e, :].bitcast(FP4X4), w4_sc[:, e * PASSES4 + a, :]
             else:
-                w, w_scale = w8_sb[a][:, e, :].bitcast(FP8X4), w8_sc[4:P, e * PASSES8 + a, :]
+                w, w_scale = w8_sb[a][:, e, :].bitcast(FP8X4), w8_sc[W8_ROW:P, e * PASSES8 + a, :]
             nc.tensor.matmul_mx(
                 out=acc[e],
                 lhsT=w,
@@ -172,81 +186,74 @@ def tile_moe_ecr_lin_gelu_kernel(
                 stop=(s == PASSES - 1),
             )
 
-        def supply(s):
-            for c in range(len(COPIES[s])):
-                interleave(s, c)
-            for t0, t1 in QUANTISE[s]:
-                quantise(s, t0, t1)
-
-        half = E // 2
         supply(0)
         gather_words(0, 0, E)
         supply(1)
         gather_scales(0, 0, E)
-        gather_words(1, 0, half)
+        gather_words(1, 0, HALF)
         supply(2)
-        gather_words(1, half, E)
+        gather_words(1, HALF, E)
         gather_words(2, 0, E)
         supply(3)
         gather_scales(1, 0, E)
-        gather_words(3, 0, half)
+        gather_words(3, 0, HALF)
         supply(4)
-        gather_words(3, half, E)
-        for s in range(3):
+        gather_words(3, HALF, E)
+        for s in range(EARLY_PASSES):
             for e in range(E):
                 multiply(s, e)
         for e0, e1 in LAST_GROUPS:
-            gather_scales(2, e0, e1)
+            gather_scales(SCALE_TILES - 1, e0, e1)
             gather_words(PASSES - 1, e0, e1)
-            for s in range(3, PASSES):
+            for s in range(EARLY_PASSES, PASSES):
                 for e in range(e0, e1):
                     multiply(s, e)
             for e in range(e0, e1):
                 nc.scalar.activation(y[:, e * C : (e + 1) * C], acc[e], GELU, bias=bias[:, e : e + 1])
 
         def weigh(r, t0, t1):
-            nc.vector.tensor_tensor(
-                prod[r][:, t0:t1], y[:].indirect(pos_sb[r][:, t0 // 16 : t1 // 16]), gate_sb[:, r, t0:t1], MULT
-            )
+            entries = pos_sb[r][:, t0 // PER_COLUMN : t1 // PER_COLUMN]
+            nc.vector.tensor_tensor(prod[r][:, t0:t1], y[:].indirect(entries), gate_sb[:, r, t0:t1], MULT)
 
         def add(dst, u, v, t0, t1):
             nc.vector.tensor_tensor(dst[:, t0:t1], u[:, t0:t1], v[:, t0:t1], ADD)
 
         def weigh_and_turn(i):
             t0, t1 = TURNED[i]
-            ps = bank(6 + i, "turn_ps%d" % i)
-            blocks = range(t0, t1, P)
+            summed = bank(E + i, "summed%d" % i)
             for r in range(TOP):
                 weigh(r, t0, t1)
-                for t in blocks:
+                for t in range(t0, t1, P):
                     nc.tensor.matmul(
-                        ps[:, t - t0 : t - t0 + P],
+                        summed[:, t - t0 : t - t0 + P],
                         lhsT=prod[r][:, t : t + P],
                         rhs=ident[:],
                         is_transpose=True,
                         start=(r == 0 and t == t0),
                         stop=(r == TOP - 1 and t == t1 - P),
                     )
-            nc.scalar.copy(turned[i][:], ps[:, 0 : t1 - t0])
+            nc.scalar.copy(turned[i][:], summed[:, 0 : t1 - t0])
 
         def turn_back(i):
             t0, t1 = TURNED[i]
-            ps = bank(i, "back_ps%d" % i)
+            back = bank(i, "back%d" % i)
             for t in range(0, t1 - t0, P):
-                nc.tensor.transpose(ps[:, t : t + P], turned[i][:, t : t + P], ident[:])
-            nc.scalar.copy(sums[i][:], ps[:, 0 : t1 - t0])
+                nc.tensor.transpose(back[:, t : t + P], turned[i][:, t : t + P], ident[:])
+            nc.scalar.copy(sums[i][:], back[:, 0 : t1 - t0])
             queue = nc.scalar if i == len(TURNED) - 1 else nc.sync
             queue.dma_start(out[:, t0:t1], sums[i][:])
 
-        bm = (b0 + b1) // 2
-        weigh_and_turn(0)
-        turn_back(0)
-        weigh_and_turn(1)
-        turn_back(1)
+        for i in range(len(TURNED)):
+            weigh_and_turn(i)
+            turn_back(i)
+
+        added0, added1 = ADDED
+        middle = (added0 + added1) // 2
+        halves = ((added0, middle), (middle, added1))
         for r in range(TOP):
-            weigh(r, b0, b1)
-        add(part, prod[0], prod[1], b0, bm)
-        add(part, prod[0], prod[1], bm, b1)
-        for t0, t1 in ((b0, bm), (bm, b1)):
+            weigh(r, added0, added1)
+        for t0, t1 in halves:
+            add(part, prod[0], prod[1], t0, t1)
+        for t0, t1 in halves:
             add(total, part, prod[2], t0, t1)
             nc.sync.dma_start(out[:, t0:t1], total[:, t0:t1])

@@ -28,9 +28,11 @@ QUADRANT = 32
 PASSES8, PASSES4 = K8 // K_PASS, (K - K8) // K_PASS
 PASSES = PASSES8 + PASSES4
 
-ORDER = [("e2m1", 0, 0, 0), ("e2m1", 1, 1, 0), ("e4m3", 0, 1, 4), ("e2m1", 2, 2, 0), ("e4m3", 1, 2, 4)]
-SCALE_TILES = PASSES4
-W8_ROW = 4
+ORDER = [("e2m1", 0, 0, 0), ("e2m1", 1, 0, 4), ("e4m3", 0, 1, 4), ("e4m3", 1, 1, 8), ("e2m1", 2, 1, 0)]
+SCALE_TILES = 2
+MOVED_PASS = 1
+LIVE_SPAN = 3 * QUADRANT + 4
+W8_ROW = 8
 
 EDGE_LOADS = [(0, 256), (256, 512), (512, 640), (640, 768)]
 MID_LOADS = [(0, 256), (256, 512), (512, 768)]
@@ -73,6 +75,7 @@ def tile_moe_ecr_lin_gelu_kernel(
         tok_scales = keep.tile([P, SCALE_TILES, WINDOW], U8, name="tok_scales", align_bytes=64)
         slot_words = [keep.tile([P, S], U32, name="slot_words%d" % s, align_bytes=64) for s in range(PASSES)]
         slot_scales = [keep.tile([P, S], U8, name="slot_scales%d" % g, align_bytes=64) for g in range(SCALE_TILES)]
+        moved_scales = keep.tile([P, S], U8, name="moved_scales", align_bytes=64)
         zeros = keep.tile([P, PAD], F32, name="zeros")
         y = keep.tile([P, S + PAD], F32, name="y")
         prod = [keep.tile([P, T], F32, name="prod%d" % r) for r in range(TOP)]
@@ -93,6 +96,7 @@ def tile_moe_ecr_lin_gelu_kernel(
         nc.vector.memset(zeros[:], 0.0)
         nc.vector.memset(tok_scales[:].rearrange("p g t -> p (g t)").bitcast(I32), 0)
         nc.vector.memset(tok_words[:, :, T:WINDOW].bitcast(I32), 0)
+        nc.vector.memset(moved_scales[:].bitcast(I32), 0)
         nc.scalar.activation(y[:, S : S + PAD], zeros[:], GELU)
 
         for s, (fmt, a, g, row) in enumerate(ORDER):
@@ -123,8 +127,8 @@ def tile_moe_ecr_lin_gelu_kernel(
         load_w4(1)
         load_scales(w8_sc, w8_scales, W8_ROW)
         load_w8(0, 0, HALF)
-        load_w4(2)
         load_w8(1, 0, HALF)
+        load_w4(2)
         nc.sync.dma_start(bias[:], b)
         load_w8(0, HALF, E)
         for e0, e1 in LAST_GROUPS[1:]:
@@ -181,7 +185,7 @@ def tile_moe_ecr_lin_gelu_kernel(
                 lhsT=w,
                 lhsT_scale=w_scale,
                 rhs=slot_words[s][:, slots].bitcast(FP8X4),
-                rhs_scale=slot_scales[g][row:P, slots],
+                rhs_scale=moved_scales[:, slots] if s == MOVED_PASS else slot_scales[g][row:P, slots],
                 start=(s == 0),
                 stop=(s == PASSES - 1),
             )
@@ -190,20 +194,21 @@ def tile_moe_ecr_lin_gelu_kernel(
         gather_words(0, 0, E)
         supply(1)
         gather_scales(0, 0, E)
-        gather_words(1, 0, HALF)
+        row = ORDER[MOVED_PASS][3]
+        nc.gpsimd.dma_start(
+            moved_scales[0:LIVE_SPAN, :].bitcast(I32), slot_scales[0][row : row + LIVE_SPAN, :].bitcast(I32)
+        )
+        gather_words(1, 0, E)
         supply(2)
-        gather_words(1, HALF, E)
         gather_words(2, 0, E)
         supply(3)
-        gather_scales(1, 0, E)
-        gather_words(3, 0, HALF)
+        gather_words(3, 0, E)
         supply(4)
-        gather_words(3, HALF, E)
         for s in range(EARLY_PASSES):
             for e in range(E):
                 multiply(s, e)
+        gather_scales(SCALE_TILES - 1, 0, E)
         for e0, e1 in LAST_GROUPS:
-            gather_scales(SCALE_TILES - 1, e0, e1)
             gather_words(PASSES - 1, e0, e1)
             for s in range(EARLY_PASSES, PASSES):
                 for e in range(e0, e1):

@@ -25,27 +25,24 @@ PACK = 4
 K_PASS = P * PACK
 PER_COLUMN = 16
 QUADRANT = 32
+ALIGN = 256
 PASSES8, PASSES4 = K8 // K_PASS, (K - K8) // K_PASS
 PASSES = PASSES8 + PASSES4
+HALF = E // 2
 
 ORDER = [("e2m1", 0, 0, 0), ("e2m1", 1, 0, 4), ("e4m3", 0, 1, 4), ("e4m3", 1, 1, 8), ("e2m1", 2, 1, 0)]
-SCALE_TILES = 2
-MOVED_PASS = 1
-LIVE_SPAN = 3 * QUADRANT + 4
+MOVED = 1
+LAST = PASSES - 1
 W8_ROW = 8
-
+LIVE_SPAN = 3 * QUADRANT + 4
 EDGE_LOADS = [(0, 256), (256, 512), (512, 640), (640, 768)]
 MID_LOADS = [(0, 256), (256, 512), (512, 768)]
 LOADS = [EDGE_LOADS, MID_LOADS, MID_LOADS, MID_LOADS, EDGE_LOADS]
-FIRST_COPIES = [(0, 256), (256, 384), (384, 512), (512, 640), (640, 768)]
-COPIES = [FIRST_COPIES] + LOADS[1:]
-ON_VECTOR = [(0, 1), (0, 4)]
+COPIES = [[(0, 256), (256, 384), (384, 512), (512, 640), (640, 768)], [(0, 256), (256, 512), (512, 608), (608, 768)]] + LOADS[2:]
+ON_VECTOR = [(0, 1), (0, 4), (1, 3)]
 QUANTISE = [EDGE_LOADS] + [[(0, 512)] + loads[2:] for loads in LOADS[1:]]
 WINDOW = 1024
-
-HALF = E // 2
 LAST_GROUPS = [(0, HALF), (HALF, E - 1), (E - 1, E)]
-EARLY_PASSES = 2
 TURNED = [(0, 256), (256, 384)]
 ADDED = (384, T)
 
@@ -58,60 +55,57 @@ def tile_moe_ecr_lin_gelu_kernel(
         keep = ctx.enter_context(tc.tile_pool(name="keep", bufs=1))
         psum = ctx.enter_context(tc.psum_pool(name="psum", bufs=1))
 
-        offs_sb = keep.tile([P, S // PER_COLUMN], U16, name="offs_sb")
-        pos_sb = [keep.tile([P, T // PER_COLUMN], U16, name="pos_sb%d" % r) for r in range(TOP)]
-        bias = keep.tile([P, E], F32, name="bias")
-        gate_sb = keep.tile([P, TOP, T], F32, name="gate_sb")
-        w8_sb = [keep.tile([P, E, 4 * N], U8, name="w8_sb%d" % a, align_bytes=64) for a in range(PASSES8)]
-        w4_sb = [keep.tile([P, E, 2 * N], U8, name="w4_sb%d" % a, align_bytes=64) for a in range(PASSES4)]
-        w8_sc = keep.tile([P, E * PASSES8, N], U8, name="w8_sc", align_bytes=64)
-        w4_sc = keep.tile([P, E * PASSES4, N], U8, name="w4_sc", align_bytes=64)
-        raw = [
-            [keep.tile([P, PACK, t1 - t0], F32, name="raw%d_%d" % (s, t0)) for t0, t1 in LOADS[s]]
-            for s in range(PASSES)
-        ]
-        grouped = [keep.tile([P, T, PACK], BF16, name="grouped%d" % s, align_bytes=64) for s in range(PASSES)]
-        tok_words = keep.tile([P, PASSES, WINDOW], U32, name="tok_words", align_bytes=64)
-        tok_scales = keep.tile([P, SCALE_TILES, WINDOW], U8, name="tok_scales", align_bytes=64)
-        slot_words = [keep.tile([P, S], U32, name="slot_words%d" % s, align_bytes=64) for s in range(PASSES)]
-        slot_scales = [keep.tile([P, S], U8, name="slot_scales%d" % g, align_bytes=64) for g in range(SCALE_TILES)]
-        moved_scales = keep.tile([P, S], U8, name="moved_scales", align_bytes=64)
-        zeros = keep.tile([P, PAD], F32, name="zeros")
-        y = keep.tile([P, S + PAD], F32, name="y")
-        prod = [keep.tile([P, T], F32, name="prod%d" % r) for r in range(TOP)]
-        part = keep.tile([P, T], F32, name="part")
-        total = keep.tile([P, T], F32, name="total")
-        ident = keep.tile([P, P], F32, name="ident")
-        turned = [keep.tile([P, t1 - t0], F32, name="turned%d" % t0) for t0, t1 in TURNED]
-        sums = [keep.tile([P, t1 - t0], F32, name="sums%d" % t0) for t0, t1 in TURNED]
+        def sbuf(shape, dtype, name, tag=None):
+            return keep.tile(shape, dtype, name=name, tag=tag or name, align_bytes=ALIGN)
 
         def bank(i, name):
             return psum.tile([P, 4 * P], F32, name=name, tag="bank%d" % i)
 
+        offs_sb = sbuf([P, S // PER_COLUMN], U16, "offs_sb")
+        pos_sb = [sbuf([P, T // PER_COLUMN], U16, "pos_sb%d" % r) for r in range(TOP)]
+        bias = sbuf([P, E], F32, "bias")
+        w8_sb = [sbuf([P, E, 4 * N], U8, "w8_sb%d" % a) for a in range(PASSES8)]
+        w4_sb = [sbuf([P, E, 2 * N], U8, "w4_sb%d" % a) for a in range(PASSES4)]
+        w8_sc = sbuf([P, E * PASSES8, N], U8, "w8_sc")
+        w4_sc = sbuf([P, E * PASSES4, N], U8, "w4_sc")
+        raw = [[sbuf([P, PACK, t1 - t0], F32, "raw%d_%d" % (s, t0)) for t0, t1 in LOADS[s]] for s in range(PASSES)]
+        grouped = [sbuf([P, T, PACK], BF16, "grouped%d" % s) for s in range(PASSES)]
+        tok_words = sbuf([P, PASSES, WINDOW], U32, "tok_words")
+        tok_scales = sbuf([P, 2, WINDOW], U8, "tok_scales")
+        slot_words = [sbuf([P, S], U32, "slot_words%d" % s) for s in range(PASSES)]
+        slot_scales = [sbuf([P, S], U8, "slot_scales%d" % g) for g in range(2)]
+        moved = sbuf([P, S], U8, "moved")
+        gate_sb = sbuf([P, TOP, T], F32, "gate_sb")
+        zeros = sbuf([P, PAD], F32, "zeros")
+        y = sbuf([P, S + PAD], F32, "y")
+        prod = [sbuf([P, T], F32, "prod%d" % r) for r in range(TOP)]
+        part = sbuf([P, T], F32, "part")
+        total = sbuf([P, T], F32, "total")
+        ident = sbuf([P, P], F32, "ident")
+        turned = [sbuf([P, t1 - t0], F32, "turned%d" % t0) for t0, t1 in TURNED]
+        sums = [sbuf([P, t1 - t0], F32, "sums%d" % t0) for t0, t1 in TURNED]
         acc = [bank(e, "acc%d" % e)[:, 0:C] for e in range(E)]
-        make_identity(nc, ident[:])
 
+        make_identity(nc, ident[:])
         nc.vector.memset(w4_sc[:].rearrange("p a n -> p (a n)").bitcast(I32), 0)
         nc.vector.memset(w8_sc[:].rearrange("p a n -> p (a n)").bitcast(I32), 0)
         nc.vector.memset(zeros[:], 0.0)
         nc.vector.memset(tok_scales[:].rearrange("p g t -> p (g t)").bitcast(I32), 0)
         nc.vector.memset(tok_words[:, :, T:WINDOW].bitcast(I32), 0)
-        nc.vector.memset(moved_scales[:].bitcast(I32), 0)
+        nc.vector.memset(moved[:].bitcast(I32), 0)
         nc.scalar.activation(y[:, S : S + PAD], zeros[:], GELU)
 
-        for s, (fmt, a, g, row) in enumerate(ORDER):
+        def load_x(s, c):
+            fmt, a, g, row = ORDER[s]
             k0 = K_PASS * a + (K8 if fmt == "e2m1" else 0)
-            for c, (t0, t1) in enumerate(LOADS[s]):
-                nc.sync.dma_start(raw[s][c][:], xT[k0 : k0 + K_PASS, t0:t1].rearrange("(p j) t -> p j t", j=PACK))
-            if s == 0:
-                nc.sync.dma_start(offs_sb[:], offs)
+            t0, t1 = LOADS[s][c]
+            nc.sync.dma_start(raw[s][c][:], xT[k0 : k0 + K_PASS, t0:t1].rearrange("(p j) t -> p j t", j=PACK))
 
-        def load_scales(sc_sb, sc, row):
-            for r in range(4):
-                nc.sync.dma_start(
-                    sc_sb[row + r : P : QUADRANT, :, :].bitcast(I32),
-                    sc[:, :, r:16:4, :].rearrange("e a q n -> q (e a) n").bitcast(I32),
-                )
+        def load_scale_rows(sc_sb, sc, row, r):
+            nc.sync.dma_start(
+                sc_sb[row + r : P : QUADRANT, :, :].bitcast(I32),
+                sc[:, :, r:16:4, :].rearrange("e a q n -> q (e a) n").bitcast(I32),
+            )
 
         def load_w4(a):
             nc.sync.dma_start(w4_sb[a][:].bitcast(I32), w4_words[:, a, :, :].rearrange("e p b -> p e b").bitcast(I32))
@@ -122,10 +116,17 @@ def tile_moe_ecr_lin_gelu_kernel(
                 w8_words[e0:e1, a, :, :, :].rearrange("e p n r -> p e (n r)").bitcast(I32),
             )
 
-        load_scales(w4_sc, w4_scales, 0)
+        for s in range(PASSES):
+            for c in range(len(LOADS[s])):
+                load_x(s, c)
+            if s == 0:
+                nc.sync.dma_start(offs_sb[:], offs)
+        for r in range(4):
+            load_scale_rows(w4_sc, w4_scales, 0, r)
         load_w4(0)
         load_w4(1)
-        load_scales(w8_sc, w8_scales, W8_ROW)
+        for r in range(4):
+            load_scale_rows(w8_sc, w8_scales, W8_ROW, r)
         load_w8(0, 0, HALF)
         load_w8(1, 0, HALF)
         load_w4(2)
@@ -150,19 +151,16 @@ def tile_moe_ecr_lin_gelu_kernel(
                 raw[s][load][:, :, t0 - base : t1 - base].rearrange("p j (c i) -> p c j i", i=4),
             )
 
-        def quantise(s, t0, t1):
-            fmt, a, g, row = ORDER[s]
-            nc.vector.quantize_mx(
-                out=tok_words[:, s, t0:t1].bitcast(FP8X4),
-                scales=tok_scales[row:P, g, t0:t1],
-                in_=grouped[s][:, t0:t1, :].rearrange("p t j -> p (t j)"),
-            )
-
         def supply(s):
+            fmt, a, g, row = ORDER[s]
             for c in range(len(COPIES[s])):
                 interleave(s, c)
             for t0, t1 in QUANTISE[s]:
-                quantise(s, t0, t1)
+                nc.vector.quantize_mx(
+                    out=tok_words[:, s, t0:t1].bitcast(FP8X4),
+                    scales=tok_scales[row:P, g, t0:t1],
+                    in_=grouped[s][:, t0:t1, :].rearrange("p t j -> p (t j)"),
+                )
 
         def slot_entries(e0, e1):
             return offs_sb[:, e0 * C // PER_COLUMN : e1 * C // PER_COLUMN]
@@ -172,6 +170,19 @@ def tile_moe_ecr_lin_gelu_kernel(
 
         def gather_scales(g, e0, e1):
             nc.vector.tensor_copy(slot_scales[g][:, e0 * C : e1 * C], tok_scales[:, g, :].indirect(slot_entries(e0, e1)))
+
+        supply(0)
+        gather_words(0, 0, E)
+        supply(1)
+        gather_scales(0, 0, E)
+        row = ORDER[MOVED][3]
+        nc.gpsimd.dma_start(moved[0:LIVE_SPAN, :].bitcast(I32), slot_scales[0][row : row + LIVE_SPAN, :].bitcast(I32))
+        gather_words(1, 0, E)
+        for s in range(2, LAST):
+            supply(s)
+            gather_words(s, 0, E)
+        supply(LAST)
+
 
         def multiply(s, e):
             fmt, a, g, row = ORDER[s]
@@ -185,34 +196,23 @@ def tile_moe_ecr_lin_gelu_kernel(
                 lhsT=w,
                 lhsT_scale=w_scale,
                 rhs=slot_words[s][:, slots].bitcast(FP8X4),
-                rhs_scale=moved_scales[:, slots] if s == MOVED_PASS else slot_scales[g][row:P, slots],
+                rhs_scale=moved[:, slots] if s == MOVED else slot_scales[g][row:P, slots],
                 start=(s == 0),
-                stop=(s == PASSES - 1),
+                stop=(s == LAST),
             )
 
-        supply(0)
-        gather_words(0, 0, E)
-        supply(1)
-        gather_scales(0, 0, E)
-        row = ORDER[MOVED_PASS][3]
-        nc.gpsimd.dma_start(
-            moved_scales[0:LIVE_SPAN, :].bitcast(I32), slot_scales[0][row : row + LIVE_SPAN, :].bitcast(I32)
-        )
-        gather_words(1, 0, E)
-        supply(2)
-        gather_words(2, 0, E)
-        supply(3)
-        gather_words(3, 0, E)
-        supply(4)
-        for s in range(EARLY_PASSES):
+        for s in (0, MOVED):
             for e in range(E):
                 multiply(s, e)
-        gather_scales(SCALE_TILES - 1, 0, E)
         for e0, e1 in LAST_GROUPS:
-            gather_words(PASSES - 1, e0, e1)
-            for s in range(EARLY_PASSES, PASSES):
-                for e in range(e0, e1):
-                    multiply(s, e)
+            if e0 % HALF == 0:
+                gather_scales(1, e0, e0 + HALF)
+                for s in (2, 3):
+                    for e in range(e0, e0 + HALF):
+                        multiply(s, e)
+            gather_words(LAST, e0, e1)
+            for e in range(e0, e1):
+                multiply(LAST, e)
             for e in range(e0, e1):
                 nc.scalar.activation(y[:, e * C : (e + 1) * C], acc[e], GELU, bias=bias[:, e : e + 1])
 
@@ -223,8 +223,7 @@ def tile_moe_ecr_lin_gelu_kernel(
         def add(dst, u, v, t0, t1):
             nc.vector.tensor_tensor(dst[:, t0:t1], u[:, t0:t1], v[:, t0:t1], ADD)
 
-        def weigh_and_turn(i):
-            t0, t1 = TURNED[i]
+        for i, (t0, t1) in enumerate(TURNED):
             summed = bank(E + i, "summed%d" % i)
             for r in range(TOP):
                 weigh(r, t0, t1)
@@ -238,19 +237,12 @@ def tile_moe_ecr_lin_gelu_kernel(
                         stop=(r == TOP - 1 and t == t1 - P),
                     )
             nc.scalar.copy(turned[i][:], summed[:, 0 : t1 - t0])
-
-        def turn_back(i):
-            t0, t1 = TURNED[i]
             back = bank(i, "back%d" % i)
             for t in range(0, t1 - t0, P):
                 nc.tensor.transpose(back[:, t : t + P], turned[i][:, t : t + P], ident[:])
             nc.scalar.copy(sums[i][:], back[:, 0 : t1 - t0])
             queue = nc.scalar if i == len(TURNED) - 1 else nc.sync
             queue.dma_start(out[:, t0:t1], sums[i][:])
-
-        for i in range(len(TURNED)):
-            weigh_and_turn(i)
-            turn_back(i)
 
         added0, added1 = ADDED
         middle = (added0 + added1) // 2

@@ -17,6 +17,7 @@ U8 = mybir.dt.uint8
 FP8X4 = mybir.dt.float8_e4m3fn_x4
 FP4X4 = mybir.dt.float4_e2m1fn_x4
 GELU = mybir.ActivationFunctionType.Gelu_apprx_tanh
+COPY = mybir.ActivationFunctionType.Copy
 MULT = mybir.AluOpType.mult
 ADD = mybir.AluOpType.add
 
@@ -79,6 +80,7 @@ def tile_moe_ecr_lin_gelu_kernel(
         zeros = sbuf([P, PAD], F32, "zeros")
         y = sbuf([P, S + PAD], F32, "y")
         prod = [sbuf([P, T], F32, "prod%d" % r) for r in range(TOP)]
+        picked = sbuf([P, T], F32, "picked")
         part = sbuf([P, T], F32, "part")
         total = sbuf([P, T], F32, "total")
         ident = sbuf([P, P], F32, "ident")
@@ -135,7 +137,7 @@ def tile_moe_ecr_lin_gelu_kernel(
         for e0, e1 in LAST_GROUPS[1:]:
             load_w8(1, e0, e1)
         first0, first1 = TURNED[0]
-        for r, pos in enumerate((pos1, pos2, pos3)):
+        for r, pos in reversed(list(enumerate((pos1, pos2, pos3)))):
             nc.sync.dma_start(pos_sb[r][:], pos)
             nc.sync.dma_start(gate_sb[:, r, first0:first1], gate[r, :, first0:first1])
         for t0, t1 in TURNED[1:] + [ADDED]:
@@ -217,15 +219,18 @@ def tile_moe_ecr_lin_gelu_kernel(
                 nc.scalar.activation(y[:, e * C : (e + 1) * C], acc[e], GELU, bias=bias[:, e : e + 1])
 
         def weigh(r, t0, t1):
-            entries = pos_sb[r][:, t0 // PER_COLUMN : t1 // PER_COLUMN]
-            nc.vector.tensor_tensor(prod[r][:, t0:t1], y[:].indirect(entries), gate_sb[:, r, t0:t1], MULT)
+            results = y[:].indirect(pos_sb[r][:, t0 // PER_COLUMN : t1 // PER_COLUMN])
+            if r == 0:
+                nc.scalar.activation(picked[:, t0:t1], results, COPY)
+                results = picked[:, t0:t1]
+            nc.vector.tensor_tensor(prod[r][:, t0:t1], results, gate_sb[:, r, t0:t1], MULT)
 
         def add(dst, u, v, t0, t1):
             nc.vector.tensor_tensor(dst[:, t0:t1], u[:, t0:t1], v[:, t0:t1], ADD)
 
         for i, (t0, t1) in enumerate(TURNED):
             summed = bank(E + i, "summed%d" % i)
-            for r in range(TOP):
+            for r in reversed(range(TOP)):
                 weigh(r, t0, t1)
                 for t in range(t0, t1, P):
                     nc.tensor.matmul(
@@ -233,8 +238,8 @@ def tile_moe_ecr_lin_gelu_kernel(
                         lhsT=prod[r][:, t : t + P],
                         rhs=ident[:],
                         is_transpose=True,
-                        start=(r == 0 and t == t0),
-                        stop=(r == TOP - 1 and t == t1 - P),
+                        start=(r == TOP - 1 and t == t0),
+                        stop=(r == 0 and t == t1 - P),
                     )
             nc.scalar.copy(turned[i][:], summed[:, 0 : t1 - t0])
             back = bank(i, "back%d" % i)
@@ -247,10 +252,10 @@ def tile_moe_ecr_lin_gelu_kernel(
         added0, added1 = ADDED
         middle = (added0 + added1) // 2
         halves = ((added0, middle), (middle, added1))
-        for r in range(TOP):
+        for r in reversed(range(TOP)):
             weigh(r, added0, added1)
         for t0, t1 in halves:
-            add(part, prod[0], prod[1], t0, t1)
+            add(part, prod[2], prod[1], t0, t1)
         for t0, t1 in halves:
-            add(total, part, prod[2], t0, t1)
+            add(total, part, prod[0], t0, t1)
             nc.sync.dma_start(out[:, t0:t1], total[:, t0:t1])

@@ -44,8 +44,7 @@ ON_VECTOR = [(0, 1), (0, 4), (1, 3)]
 QUANTISE = [EDGE_LOADS] + [[(0, 512)] + loads[2:] for loads in LOADS[1:]]
 WINDOW = 1024
 LAST_GROUPS = [(0, HALF), (HALF, E - 1), (E - 1, E)]
-TURNED = [(0, 256), (256, 384)]
-ADDED = (384, T)
+WHOLE, PARTLY, PLAIN = (0, 256), (256, 384), (384, T)
 
 
 def tile_moe_ecr_lin_gelu_kernel(
@@ -84,8 +83,7 @@ def tile_moe_ecr_lin_gelu_kernel(
         part = sbuf([P, T], F32, "part")
         total = sbuf([P, T], F32, "total")
         ident = sbuf([P, P], F32, "ident")
-        turned = [sbuf([P, t1 - t0], F32, "turned%d" % t0) for t0, t1 in TURNED]
-        sums = [sbuf([P, t1 - t0], F32, "sums%d" % t0) for t0, t1 in TURNED]
+        turned = [sbuf([P, t1 - t0], F32, "turned%d" % t0) for t0, t1 in (WHOLE, PARTLY)]
         acc = [bank(e, "acc%d" % e)[:, 0:C] for e in range(E)]
 
         make_identity(nc, ident[:])
@@ -136,12 +134,15 @@ def tile_moe_ecr_lin_gelu_kernel(
         load_w8(0, HALF, E)
         for e0, e1 in LAST_GROUPS[1:]:
             load_w8(1, e0, e1)
-        first0, first1 = TURNED[0]
+        def load_gates(r0, r1, t0, t1):
+            nc.sync.dma_start(gate_sb[:, r0:r1, t0:t1], gate[r0:r1, :, t0:t1].rearrange("r n t -> n r t"))
+
         for r, pos in reversed(list(enumerate((pos1, pos2, pos3)))):
             nc.sync.dma_start(pos_sb[r][:], pos)
-            nc.sync.dma_start(gate_sb[:, r, first0:first1], gate[r, :, first0:first1])
-        for t0, t1 in TURNED[1:] + [ADDED]:
-            nc.sync.dma_start(gate_sb[:, :, t0:t1], gate[:, :, t0:t1].rearrange("r n t -> n r t"))
+            load_gates(r, r + 1, *WHOLE)
+        load_gates(1, TOP, *PARTLY)
+        load_gates(1, TOP, *PLAIN)
+        load_gates(0, 1, PARTLY[0], T)
 
         def interleave(s, c):
             t0, t1 = COPIES[s][c]
@@ -225,12 +226,9 @@ def tile_moe_ecr_lin_gelu_kernel(
                 results = picked[:, t0:t1]
             nc.vector.tensor_tensor(prod[r][:, t0:t1], results, gate_sb[:, r, t0:t1], MULT)
 
-        def add(dst, u, v, t0, t1):
-            nc.vector.tensor_tensor(dst[:, t0:t1], u[:, t0:t1], v[:, t0:t1], ADD)
-
-        for i, (t0, t1) in enumerate(TURNED):
+        def sum_turned(i, lists, t0, t1):
             summed = bank(E + i, "summed%d" % i)
-            for r in reversed(range(TOP)):
+            for r in lists:
                 weigh(r, t0, t1)
                 for t in range(t0, t1, P):
                     nc.tensor.matmul(
@@ -238,24 +236,30 @@ def tile_moe_ecr_lin_gelu_kernel(
                         lhsT=prod[r][:, t : t + P],
                         rhs=ident[:],
                         is_transpose=True,
-                        start=(r == TOP - 1 and t == t0),
-                        stop=(r == 0 and t == t1 - P),
+                        start=(r == lists[0] and t == t0),
+                        stop=(r == lists[-1] and t == t1 - P),
                     )
             nc.scalar.copy(turned[i][:], summed[:, 0 : t1 - t0])
             back = bank(i, "back%d" % i)
             for t in range(0, t1 - t0, P):
                 nc.tensor.transpose(back[:, t : t + P], turned[i][:, t : t + P], ident[:])
-            nc.scalar.copy(sums[i][:], back[:, 0 : t1 - t0])
-            queue = nc.scalar if i == len(TURNED) - 1 else nc.sync
-            queue.dma_start(out[:, t0:t1], sums[i][:])
+            return back[:, 0 : t1 - t0]
 
-        added0, added1 = ADDED
-        middle = (added0 + added1) // 2
-        halves = ((added0, middle), (middle, added1))
-        for r in reversed(range(TOP)):
-            weigh(r, added0, added1)
-        for t0, t1 in halves:
-            add(part, prod[2], prod[1], t0, t1)
-        for t0, t1 in halves:
-            add(total, part, prod[0], t0, t1)
+        def finish(others, t0, t1):
+            nc.vector.tensor_tensor(total[:, t0:t1], prod[0][:, t0:t1], others, ADD)
             nc.sync.dma_start(out[:, t0:t1], total[:, t0:t1])
+
+        t0, t1 = WHOLE
+        nc.scalar.copy(total[:, t0:t1], sum_turned(0, (2, 1, 0), t0, t1))
+        nc.scalar.dma_start(out[:, t0:t1], total[:, t0:t1])
+        partly = sum_turned(1, (2, 1), *PARTLY)
+        t0, t1 = PLAIN
+        weigh(2, t0, t1)
+        weigh(1, t0, t1)
+        middle = t1 - P
+        weigh(0, PARTLY[0], middle)
+        nc.vector.tensor_tensor(part[:, t0:t1], prod[2][:, t0:t1], prod[1][:, t0:t1], ADD)
+        finish(partly, *PARTLY)
+        weigh(0, middle, t1)
+        finish(part[:, t0:middle], t0, middle)
+        finish(part[:, middle:t1], middle, t1)

@@ -38,7 +38,7 @@ W8_ROW = 8
 LIVE_SPAN = 3 * QUADRANT + 4
 EDGE_LOADS = [(0, 256), (256, 512), (512, 640), (640, 768)]
 MID_LOADS = [(0, 256), (256, 512), (512, 768)]
-LOADS = [EDGE_LOADS, MID_LOADS, MID_LOADS, MID_LOADS, EDGE_LOADS]
+LOADS = [MID_LOADS, MID_LOADS, MID_LOADS, MID_LOADS, EDGE_LOADS]
 COPIES = [[(0, 256), (256, 384), (384, 512), (512, 640), (640, 768)], [(0, 256), (256, 512), (512, 608), (608, 768)]] + LOADS[2:]
 ON_VECTOR = [(0, 1), (0, 4), (1, 3)]
 QUANTISE = [EDGE_LOADS] + [[(0, 512)] + loads[2:] for loads in LOADS[1:]]

@@ -86,13 +86,13 @@ def tile_moe_ecr_lin_gelu_kernel(
         turned = [sbuf([P, t1 - t0], F32, "turned%d" % t0) for t0, t1 in (WHOLE, PARTLY)]
         acc = [bank(e, "acc%d" % e)[:, 0:C] for e in range(E)]
 
-        make_identity(nc, ident[:])
         nc.vector.memset(w4_sc[:].rearrange("p a n -> p (a n)").bitcast(I32), 0)
         nc.vector.memset(w8_sc[:].rearrange("p a n -> p (a n)").bitcast(I32), 0)
-        nc.vector.memset(zeros[:], 0.0)
-        nc.vector.memset(tok_scales[:].rearrange("p g t -> p (g t)").bitcast(I32), 0)
-        nc.vector.memset(tok_words[:, :, T:WINDOW].bitcast(I32), 0)
-        nc.vector.memset(moved[:].bitcast(I32), 0)
+        nc.gpsimd.memset(zeros[:], 0.0)
+        nc.gpsimd.memset(tok_scales[:].rearrange("p g t -> p (g t)").bitcast(I32), 0)
+        nc.gpsimd.memset(tok_words[:, :, T:WINDOW].bitcast(I32), 0)
+        nc.gpsimd.memset(moved[:].bitcast(I32), 0)
+        make_identity(nc, ident[:])
         nc.scalar.activation(y[:, S : S + PAD], zeros[:], GELU)
 
         def load_x(s, c):
@@ -247,7 +247,7 @@ def tile_moe_ecr_lin_gelu_kernel(
 
         def finish(others, t0, t1):
             nc.vector.tensor_tensor(total[:, t0:t1], prod[0][:, t0:t1], others, ADD)
-            nc.sync.dma_start(out[:, t0:t1], total[:, t0:t1])
+            nc.scalar.dma_start(out[:, t0:t1], total[:, t0:t1])
 
         t0, t1 = WHOLE
         nc.scalar.copy(total[:, t0:t1], sum_turned(0, (2, 1, 0), t0, t1))

@@ -39,9 +39,12 @@ LIVE_SPAN = 3 * QUADRANT + 4
 EDGE_LOADS = [(0, 256), (256, 512), (512, 640), (640, 768)]
 MID_LOADS = [(0, 256), (256, 512), (512, 768)]
 LOADS = [MID_LOADS, MID_LOADS, MID_LOADS, MID_LOADS, EDGE_LOADS]
-COPIES = [[(0, 256), (256, 384), (384, 512), (512, 640), (640, 768)], [(0, 256), (256, 512), (512, 608), (608, 768)]] + LOADS[2:]
-ON_VECTOR = [(0, 1), (0, 4), (1, 3)]
-QUANTISE = [EDGE_LOADS] + [[(0, 512)] + loads[2:] for loads in LOADS[1:]]
+FIRST_COPIES = [(0, 256, "scalar"), (256, 384, "vector"), (384, 512, "scalar"), (512, 640, "scalar"), (640, 768, "vector")]
+SECOND_COPIES = [(0, 128, "gpsimd"), (128, 256, "scalar"), (256, 512, "scalar"), (512, 608, "scalar"), (608, 768, "vector")]
+LATER_COPIES = [(0, 128, "gpsimd"), (128, 256, "scalar"), (256, 512, "scalar"), (512, 640, "scalar"), (640, 768, "scalar")]
+COPIES = [FIRST_COPIES, SECOND_COPIES, LATER_COPIES, LATER_COPIES, LATER_COPIES]
+LATER_QUANTISE = [(0, 128), (128, 640), (640, 768)]
+QUANTISE = [EDGE_LOADS, [(0, 128), (128, 256), (256, 512), (512, 768)]] + [LATER_QUANTISE] * 3
 WINDOW = 1024
 LAST_GROUPS = [(0, HALF), (HALF, E - 1), (E - 1, E)]
 WHOLE, PARTLY, PLAIN = (0, 256), (256, 384), (384, T)
@@ -69,12 +72,11 @@ def tile_moe_ecr_lin_gelu_kernel(
         w8_sc = sbuf([P, E * PASSES8, N], U8, "w8_sc")
         w4_sc = sbuf([P, E * PASSES4, N], U8, "w4_sc")
         raw = [[sbuf([P, PACK, t1 - t0], F32, "raw%d_%d" % (s, t0)) for t0, t1 in LOADS[s]] for s in range(PASSES)]
-        grouped = [sbuf([P, T, PACK], BF16, "grouped%d" % s) for s in range(PASSES)]
-        tok_words = sbuf([P, PASSES, WINDOW], U32, "tok_words")
-        tok_scales = sbuf([P, 2, WINDOW], U8, "tok_scales")
+        grouped = dict()
+        tok_words = sbuf([P, (PASSES - 1) * T + WINDOW], U32, "tok_words")
+        tok_scales = sbuf([P, T + WINDOW], U8, "tok_scales")
         slot_words = [sbuf([P, S], U32, "slot_words%d" % s) for s in range(PASSES)]
         slot_scales = [sbuf([P, S], U8, "slot_scales%d" % g) for g in range(2)]
-        moved = sbuf([P, S], U8, "moved")
         gate_sb = sbuf([P, TOP, T], F32, "gate_sb")
         zeros = sbuf([P, PAD], F32, "zeros")
         y = sbuf([P, S + PAD], F32, "y")
@@ -86,12 +88,11 @@ def tile_moe_ecr_lin_gelu_kernel(
         turned = [sbuf([P, t1 - t0], F32, "turned%d" % t0) for t0, t1 in (WHOLE, PARTLY)]
         acc = [bank(e, "acc%d" % e)[:, 0:C] for e in range(E)]
 
-        nc.vector.memset(w4_sc[:].rearrange("p a n -> p (a n)").bitcast(I32), 0)
-        nc.vector.memset(w8_sc[:].rearrange("p a n -> p (a n)").bitcast(I32), 0)
+        nc.gpsimd.memset(w4_sc[:].rearrange("p a n -> p (a n)").bitcast(I32), 0)
+        nc.gpsimd.memset(w8_sc[:].rearrange("p a n -> p (a n)").bitcast(I32), 0)
         nc.gpsimd.memset(zeros[:], 0.0)
-        nc.gpsimd.memset(tok_scales[:].rearrange("p g t -> p (g t)").bitcast(I32), 0)
-        nc.gpsimd.memset(tok_words[:, :, T:WINDOW].bitcast(I32), 0)
-        nc.gpsimd.memset(moved[:].bitcast(I32), 0)
+        nc.gpsimd.memset(tok_scales[:].bitcast(I32), 0)
+        nc.gpsimd.memset(tok_words[:, PASSES * T :].bitcast(I32), 0)
         make_identity(nc, ident[:])
         nc.scalar.activation(y[:, S : S + PAD], zeros[:], GELU)
 
@@ -144,41 +145,45 @@ def tile_moe_ecr_lin_gelu_kernel(
         load_gates(1, TOP, *PLAIN)
         load_gates(0, 1, PARTLY[0], T)
 
-        def interleave(s, c):
-            t0, t1 = COPIES[s][c]
-            load = max(i for i, (u0, u1) in enumerate(LOADS[s]) if u0 <= t0)
-            base = LOADS[s][load][0]
-            copy = nc.vector.tensor_copy if (s, c) in ON_VECTOR else nc.scalar.copy
-            copy(
-                grouped[s][:, t0:t1, :].rearrange("p (c i) j -> p c j i", i=4),
-                raw[s][load][:, :, t0 - base : t1 - base].rearrange("p j (c i) -> p c j i", i=4),
-            )
-
         def supply(s):
             fmt, a, g, row = ORDER[s]
-            for c in range(len(COPIES[s])):
-                interleave(s, c)
+            for t0, t1 in QUANTISE[s]:
+                handed_over = s > 0 and t0 == 0
+                tag = "grouped%d_%d" % ((s - 1, QUANTISE[s - 1][-1][0]) if handed_over else (s, t0))
+                grouped[s, t0] = sbuf([P, t1 - t0, PACK], BF16, "grouped%d_%d" % (s, t0), tag=tag)
+            for t0, t1, engine in COPIES[s]:
+                load = max(i for i, (u0, u1) in enumerate(LOADS[s]) if u0 <= t0)
+                base = LOADS[s][load][0]
+                piece = max(u0 for u0, u1 in QUANTISE[s] if u0 <= t0)
+                target = grouped[s, piece][:, t0 - piece : t1 - piece, :]
+                source = raw[s][load][:, :, t0 - base : t1 - base]
+                if engine == "gpsimd":
+                    nc.gpsimd.tensor_copy(target, source.rearrange("p j t -> p t j"))
+                else:
+                    copy = nc.vector.tensor_copy if engine == "vector" else nc.scalar.copy
+                    copy(target.rearrange("p (c i) j -> p c j i", i=4), source.rearrange("p j (c i) -> p c j i", i=4))
             for t0, t1 in QUANTISE[s]:
                 nc.vector.quantize_mx(
-                    out=tok_words[:, s, t0:t1].bitcast(FP8X4),
-                    scales=tok_scales[row:P, g, t0:t1],
-                    in_=grouped[s][:, t0:t1, :].rearrange("p t j -> p (t j)"),
+                    out=tok_words[:, (LAST - s) * T + t0 : (LAST - s) * T + t1].bitcast(FP8X4),
+                    scales=tok_scales[row:P, (1 - g) * T + t0 : (1 - g) * T + t1],
+                    in_=grouped[s, t0][:].rearrange("p t j -> p (t j)"),
                 )
 
         def slot_entries(e0, e1):
             return offs_sb[:, e0 * C // PER_COLUMN : e1 * C // PER_COLUMN]
 
         def gather_words(s, e0, e1):
-            nc.vector.tensor_copy(slot_words[s][:, e0 * C : e1 * C], tok_words[:, s, :].indirect(slot_entries(e0, e1)))
+            nc.vector.tensor_copy(slot_words[s][:, e0 * C : e1 * C], tok_words[:, (LAST - s) * T : (LAST - s) * T + WINDOW].indirect(slot_entries(e0, e1)))
 
         def gather_scales(g, e0, e1):
-            nc.vector.tensor_copy(slot_scales[g][:, e0 * C : e1 * C], tok_scales[:, g, :].indirect(slot_entries(e0, e1)))
+            nc.vector.tensor_copy(slot_scales[g][:, e0 * C : e1 * C], tok_scales[:, (1 - g) * T : (1 - g) * T + WINDOW].indirect(slot_entries(e0, e1)))
 
         supply(0)
         gather_words(0, 0, E)
         supply(1)
         gather_scales(0, 0, E)
         row = ORDER[MOVED][3]
+        moved = sbuf([P, S], U8, "moved", tag="raw0_0")
         nc.gpsimd.dma_start(moved[0:LIVE_SPAN, :].bitcast(I32), slot_scales[0][row : row + LIVE_SPAN, :].bitcast(I32))
         gather_words(1, 0, E)
         for s in range(2, LAST):

from contextlib import ExitStack

import concourse.mybir as mybir
from concourse.masks import make_identity

K, T, E, C, N = 2560, 768, 6, 128, 128
TOP, PAD, K8 = 3, 64, 1024
S = E * C
FLOPS = 2 * K * S * N

F32 = mybir.dt.float32
BF16 = mybir.dt.bfloat16
I32 = mybir.dt.int32
U32 = mybir.dt.uint32
U16 = mybir.dt.uint16
U8 = mybir.dt.uint8
FP8X4 = mybir.dt.float8_e4m3fn_x4
FP4X4 = mybir.dt.float4_e2m1fn_x4
GELU = mybir.ActivationFunctionType.Gelu_apprx_tanh
COPY = mybir.ActivationFunctionType.Copy
MULT = mybir.AluOpType.mult
ADD = mybir.AluOpType.add

P = 128
PACK = 4
K_PASS = P * PACK
PER_COLUMN = 16
QUADRANT = 32
ALIGN = 256
PASSES8, PASSES4 = K8 // K_PASS, (K - K8) // K_PASS
PASSES = PASSES8 + PASSES4
HALF = E // 2

ORDER = [("e2m1", 0, 0, 0), ("e2m1", 1, 0, 4), ("e4m3", 0, 1, 4), ("e4m3", 1, 1, 8), ("e2m1", 2, 1, 0)]
MOVED = 1
LAST = PASSES - 1
W8_ROW = 8
LIVE_SPAN = 3 * QUADRANT + 4
EDGE_LOADS = [(0, 256), (256, 512), (512, 640), (640, 768)]
MID_LOADS = [(0, 256), (256, 512), (512, 768)]
LOADS = [MID_LOADS, MID_LOADS, MID_LOADS, MID_LOADS, EDGE_LOADS]
FIRST_COPIES = [(0, 256, "scalar"), (256, 384, "vector"), (384, 512, "scalar"), (512, 640, "scalar"), (640, 768, "vector")]
SECOND_COPIES = [(0, 128, "gpsimd"), (128, 256, "scalar"), (256, 512, "scalar"), (512, 608, "scalar"), (608, 768, "vector")]
LATER_COPIES = [(0, 128, "gpsimd"), (128, 256, "scalar"), (256, 512, "scalar"), (512, 640, "scalar"), (640, 768, "scalar")]
COPIES = [FIRST_COPIES, SECOND_COPIES, LATER_COPIES, LATER_COPIES, LATER_COPIES]
LATER_QUANTISE = [(0, 128), (128, 640), (640, 768)]
QUANTISE = [EDGE_LOADS, [(0, 128), (128, 256), (256, 512), (512, 768)]] + [LATER_QUANTISE] * 3
WINDOW = 1024
LAST_GROUPS = [(0, HALF), (HALF, E - 1), (E - 1, E)]
WHOLE, PARTLY, PLAIN = (0, 256), (256, 384), (384, T)


def tile_moe_ecr_lin_gelu_kernel(
    tc, xT, w8_words, w8_scales, w4_words, w4_scales, b, gate, offs, pos1, pos2, pos3, out
):
    nc = tc.nc
    with ExitStack() as ctx:
        keep = ctx.enter_context(tc.tile_pool(name="keep", bufs=1))
        psum = ctx.enter_context(tc.psum_pool(name="psum", bufs=1))

        def sbuf(shape, dtype, name, tag=None):
            return keep.tile(shape, dtype, name=name, tag=tag or name, align_bytes=ALIGN)

        def bank(i, name):
            return psum.tile([P, 4 * P], F32, name=name, tag="bank%d" % i)

        offs_sb = sbuf([P, S // PER_COLUMN], U16, "offs_sb")
        pos_sb = [sbuf([P, T // PER_COLUMN], U16, "pos_sb%d" % r) for r in range(TOP)]
        bias = sbuf([P, E], F32, "bias")
        w8_sb = [sbuf([P, E, 4 * N], U8, "w8_sb%d" % a) for a in range(PASSES8)]
        w4_sb = [sbuf([P, E, 2 * N], U8, "w4_sb%d" % a) for a in range(PASSES4)]
        w8_sc = sbuf([P, E * PASSES8, N], U8, "w8_sc")
        w4_sc = sbuf([P, E * PASSES4, N], U8, "w4_sc")
        raw = [[sbuf([P, PACK, t1 - t0], F32, "raw%d_%d" % (s, t0)) for t0, t1 in LOADS[s]] for s in range(PASSES)]
        grouped = dict()
        tok_words = sbuf([P, (PASSES - 1) * T + WINDOW], U32, "tok_words")
        tok_scales = sbuf([P, T + WINDOW], U8, "tok_scales")
        slot_words = [sbuf([P, S], U32, "slot_words%d" % s) for s in range(PASSES)]
        slot_scales = [sbuf([P, S], U8, "slot_scales%d" % g) for g in range(2)]
        gate_sb = sbuf([P, TOP, T], F32, "gate_sb")
        zeros = sbuf([P, PAD], F32, "zeros")
        y = sbuf([P, S + PAD], F32, "y")
        prod = [sbuf([P, T], F32, "prod%d" % r) for r in range(TOP)]
        picked = sbuf([P, T], F32, "picked")
        part = sbuf([P, T], F32, "part")
        total = sbuf([P, T], F32, "total")
        ident = sbuf([P, P], F32, "ident")
        turned = [sbuf([P, t1 - t0], F32, "turned%d" % t0) for t0, t1 in (WHOLE, PARTLY)]
        acc = [bank(e, "acc%d" % e)[:, 0:C] for e in range(E)]

        nc.gpsimd.memset(w4_sc[:].rearrange("p a n -> p (a n)").bitcast(I32), 0)
        nc.gpsimd.memset(w8_sc[:].rearrange("p a n -> p (a n)").bitcast(I32), 0)
        nc.gpsimd.memset(zeros[:], 0.0)
        nc.gpsimd.memset(tok_scales[:].bitcast(I32), 0)
        nc.gpsimd.memset(tok_words[:, PASSES * T :].bitcast(I32), 0)
        make_identity(nc, ident[:])
        nc.scalar.activation(y[:, S : S + PAD], zeros[:], GELU)

        def load_x(s, c):
            fmt, a, g, row = ORDER[s]
            k0 = K_PASS * a + (K8 if fmt == "e2m1" else 0)
            t0, t1 = LOADS[s][c]
            nc.sync.dma_start(raw[s][c][:], xT[k0 : k0 + K_PASS, t0:t1].rearrange("(p j) t -> p j t", j=PACK))

        def load_scale_rows(sc_sb, sc, row, r):
            nc.sync.dma_start(
                sc_sb[row + r : P : QUADRANT, :, :].bitcast(I32),
                sc[:, :, r:16:4, :].rearrange("e a q n -> q (e a) n").bitcast(I32),
            )

        def load_w4(a):
            nc.sync.dma_start(w4_sb[a][:].bitcast(I32), w4_words[:, a, :, :].rearrange("e p b -> p e b").bitcast(I32))

        def load_w8(a, e0, e1):
            nc.sync.dma_start(
                w8_sb[a][:, e0:e1, :].bitcast(I32),
                w8_words[e0:e1, a, :, :, :].rearrange("e p n r -> p e (n r)").bitcast(I32),
            )

        for s in range(PASSES):
            for c in range(len(LOADS[s])):
                load_x(s, c)
            if s == 0:
                nc.sync.dma_start(offs_sb[:], offs)
        for r in range(4):
            load_scale_rows(w4_sc, w4_scales, 0, r)
        load_w4(0)
        load_w4(1)
        for r in range(4):
            load_scale_rows(w8_sc, w8_scales, W8_ROW, r)
        load_w8(0, 0, HALF)
        load_w8(1, 0, HALF)
        load_w4(2)
        nc.sync.dma_start(bias[:], b)
        load_w8(0, HALF, E)
        for e0, e1 in LAST_GROUPS[1:]:
            load_w8(1, e0, e1)
        def load_gates(r0, r1, t0, t1):
            nc.sync.dma_start(gate_sb[:, r0:r1, t0:t1], gate[r0:r1, :, t0:t1].rearrange("r n t -> n r t"))

        for r, pos in reversed(list(enumerate((pos1, pos2, pos3)))):
            nc.sync.dma_start(pos_sb[r][:], pos)
            load_gates(r, r + 1, *WHOLE)
        load_gates(1, TOP, *PARTLY)
        load_gates(1, TOP, *PLAIN)
        load_gates(0, 1, PARTLY[0], T)

        def supply(s):
            fmt, a, g, row = ORDER[s]
            for t0, t1 in QUANTISE[s]:
                handed_over = s > 0 and t0 == 0
                tag = "grouped%d_%d" % ((s - 1, QUANTISE[s - 1][-1][0]) if handed_over else (s, t0))
                grouped[s, t0] = sbuf([P, t1 - t0, PACK], BF16, "grouped%d_%d" % (s, t0), tag=tag)
            for t0, t1, engine in COPIES[s]:
                load = max(i for i, (u0, u1) in enumerate(LOADS[s]) if u0 <= t0)
                base = LOADS[s][load][0]
                piece = max(u0 for u0, u1 in QUANTISE[s] if u0 <= t0)
                target = grouped[s, piece][:, t0 - piece : t1 - piece, :]
                source = raw[s][load][:, :, t0 - base : t1 - base]
                if engine == "gpsimd":
                    nc.gpsimd.tensor_copy(target, source.rearrange("p j t -> p t j"))
                else:
                    copy = nc.vector.tensor_copy if engine == "vector" else nc.scalar.copy
                    copy(target.rearrange("p (c i) j -> p c j i", i=4), source.rearrange("p j (c i) -> p c j i", i=4))
            for t0, t1 in QUANTISE[s]:
                nc.vector.quantize_mx(
                    out=tok_words[:, (LAST - s) * T + t0 : (LAST - s) * T + t1].bitcast(FP8X4),
                    scales=tok_scales[row:P, (1 - g) * T + t0 : (1 - g) * T + t1],
                    in_=grouped[s, t0][:].rearrange("p t j -> p (t j)"),
                )

        def slot_entries(e0, e1):
            return offs_sb[:, e0 * C // PER_COLUMN : e1 * C // PER_COLUMN]

        def gather_words(s, e0, e1):
            nc.vector.tensor_copy(slot_words[s][:, e0 * C : e1 * C], tok_words[:, (LAST - s) * T : (LAST - s) * T + WINDOW].indirect(slot_entries(e0, e1)))

        def gather_scales(g, e0, e1):
            nc.vector.tensor_copy(slot_scales[g][:, e0 * C : e1 * C], tok_scales[:, (1 - g) * T : (1 - g) * T + WINDOW].indirect(slot_entries(e0, e1)))

        supply(0)
        gather_words(0, 0, E)
        supply(1)
        gather_scales(0, 0, E)
        row = ORDER[MOVED][3]
        moved = sbuf([P, S], U8, "moved", tag="raw0_0")
        nc.gpsimd.dma_start(moved[0:LIVE_SPAN, :].bitcast(I32), slot_scales[0][row : row + LIVE_SPAN, :].bitcast(I32))
        gather_words(1, 0, E)
        for s in range(2, LAST):
            supply(s)
            gather_words(s, 0, E)
        supply(LAST)


        def multiply(s, e):
            fmt, a, g, row = ORDER[s]
            slots = slice(e * C, (e + 1) * C)
            if fmt == "e2m1":
                w, w_scale = w4_sb[a][:, e, :].bitcast(FP4X4), w4_sc[:, e * PASSES4 + a, :]
            else:
                w, w_scale = w8_sb[a][:, e, :].bitcast(FP8X4), w8_sc[W8_ROW:P, e * PASSES8 + a, :]
            nc.tensor.matmul_mx(
                out=acc[e],
                lhsT=w,
                lhsT_scale=w_scale,
                rhs=slot_words[s][:, slots].bitcast(FP8X4),
                rhs_scale=moved[:, slots] if s == MOVED else slot_scales[g][row:P, slots],
                start=(s == 0),
                stop=(s == LAST),
            )

        for s in (0, MOVED):
            for e in range(E):
                multiply(s, e)
        for e0, e1 in LAST_GROUPS:
            if e0 % HALF == 0:
                gather_scales(1, e0, e0 + HALF)
                for s in (2, 3):
                    for e in range(e0, e0 + HALF):
                        multiply(s, e)
            gather_words(LAST, e0, e1)
            for e in range(e0, e1):
                multiply(LAST, e)
            for e in range(e0, e1):
                nc.scalar.activation(y[:, e * C : (e + 1) * C], acc[e], GELU, bias=bias[:, e : e + 1])

        def weigh(r, t0, t1):
            results = y[:].indirect(pos_sb[r][:, t0 // PER_COLUMN : t1 // PER_COLUMN])
            if r == 0:
                nc.scalar.activation(picked[:, t0:t1], results, COPY)
                results = picked[:, t0:t1]
            nc.vector.tensor_tensor(prod[r][:, t0:t1], results, gate_sb[:, r, t0:t1], MULT)

        def sum_turned(i, lists, t0, t1):
            summed = bank(E + i, "summed%d" % i)
            for r in lists:
                weigh(r, t0, t1)
                for t in range(t0, t1, P):
                    nc.tensor.matmul(
                        summed[:, t - t0 : t - t0 + P],
                        lhsT=prod[r][:, t : t + P],
                        rhs=ident[:],
                        is_transpose=True,
                        start=(r == lists[0] and t == t0),
                        stop=(r == lists[-1] and t == t1 - P),
                    )
            nc.scalar.copy(turned[i][:], summed[:, 0 : t1 - t0])
            back = bank(i, "back%d" % i)
            for t in range(0, t1 - t0, P):
                nc.tensor.transpose(back[:, t : t + P], turned[i][:, t : t + P], ident[:])
            return back[:, 0 : t1 - t0]

        def finish(others, t0, t1):
            nc.vector.tensor_tensor(total[:, t0:t1], prod[0][:, t0:t1], others, ADD)
            nc.scalar.dma_start(out[:, t0:t1], total[:, t0:t1])

        t0, t1 = WHOLE
        nc.scalar.copy(total[:, t0:t1], sum_turned(0, (2, 1, 0), t0, t1))
        nc.scalar.dma_start(out[:, t0:t1], total[:, t0:t1])
        partly = sum_turned(1, (2, 1), *PARTLY)
        t0, t1 = PLAIN
        weigh(2, t0, t1)
        weigh(1, t0, t1)
        middle = t1 - P
        weigh(0, PARTLY[0], middle)
        nc.vector.tensor_tensor(part[:, t0:t1], prod[2][:, t0:t1], prod[1][:, t0:t1], ADD)
        finish(partly, *PARTLY)
        weigh(0, middle, t1)
        finish(part[:, t0:middle], t0, middle)
        finish(part[:, middle:t1], middle, t1)
